import numpy as np, ml_dtypes
CORES = [3,11,19,27,35,43,51,59]
N = 8
BF = ml_dtypes.bfloat16
W, K, RO = 6144, 128, 4
M = N * K
def rows(rng, n):
    return np.argsort(rng.random(n.shape + (16,)), axis=-1) < n[..., None]
def swaps(rng, q, k):
    u = np.argsort(rng.random((k.size, 2, 8)), axis=-1) < k[:, None, None]
    a = np.zeros((k.size, 16), bool); a[:, q] = u[:, 0]; a[:, ~q] = u[:, 1]
    return a
def off(rng, q, lo, hi):
    e = rng.integers(lo, hi, q.shape); up = rng.random(q.shape) < 0.5
    return np.where((up & (q + e <= 63)) | (q - e < 0), q + e, q - e)
def mix(rng, q, far, lo, hi):
    y = np.broadcast_to(q, far.shape + (16,))
    return np.where(rows(rng, far), off(rng, y, lo, hi), y)
def put(x, r, g, p, v):
    x[r, g, 2 * p] = v; x[r, g, 2 * p + 1] = v
def names(rng, lim=W // 2):
    p = np.argsort(rng.random((8, 16, W // 2)) + 2.0 * (np.arange(W // 2) >= lim), axis=-1)[..., :M]
    return np.ascontiguousarray((2 * p + rng.integers(0, 2, p.shape)).reshape(8, 16, N, K).transpose(2, 0, 1, 3))
def spots(rng, pairs, alike):
    p = np.repeat(pairs[:, None], 16, axis=1); q = np.take_along_axis(p, np.argsort(rng.random(p.shape), axis=-1), -1)
    for g in alike: q[g] = p[g]
    return np.ascontiguousarray((2 * q + rng.integers(0, 2, q.shape)).transpose(2, 0, 1, 3))
def lay(pairs, rec, rest):
    z = rest.copy()
    for g in range(8): z[:, g, pairs[g].reshape(-1)] = rec[:, g]
    return np.repeat(z, 2, axis=2)
def near(rng, a, p, amp=1):
    a = np.broadcast_to(a, (N, 8, W, 16)); e = np.where(rng.random(a.shape) < 0.5, 1, rng.integers(2, 6, a.shape)) * (2 * rng.integers(0, 2, a.shape) - 1)
    return np.clip(a + amp * e * (rng.random(a.shape) < p), 0, 63)
def pack(fa, cl, ru):
    b = np.ascontiguousarray(ru.transpose(0, 2, 1)).reshape(128, 16).astype(np.float32).astype(BF)
    return {"fa": np.ascontiguousarray(fa.transpose(0, 1, 3, 2)).reshape(N, 128, W).astype(np.float32).astype(BF),
            "cl": np.ascontiguousarray(cl).reshape(N, 128, K).astype(np.int32), "ru": np.stack([b] * N)}
def setup_inputs(rng):
    a = rng.integers(1, 63, (8, 16)); e = (rng.random((N, 8, 16)) < 0.12) * (2 * rng.integers(0, 2, (N, 8, 16)) - 1)
    fa = near(rng, (a + e)[:, :, None], 0.3 + 0.6 * rng.random((N, 8, W, 1)))
    ru = np.clip(a[:, None] + (rng.random((8, 16, 16)) < 0.1) * (2 * rng.integers(0, 2, (8, 16, 16)) - 1), 0, 63)
    return pack(fa, names(rng), ru)
def setup_inputs_spread(rng):
    a = rng.integers(0, 64, (1, 8, 1, 16)); e = (rng.random((N, 8, 1, 16)) < 0.12) * (2 * rng.integers(0, 2, (N, 8, 1, 16)) - 1)
    fa = near(rng, np.clip(a + e, 0, 63), rng.random((N, 8, W, 1)) ** 2 + 0.1, 2 ** rng.integers(0, 5, (N, 8, W, 1)))
    s = np.where(rng.random((N, 4, W, 1)) < 0.6, 16, rng.choice(np.array([1, 3, 8]), (N, 4, W, 1)))
    u = np.minimum((64 * rng.random((N, 4, W, 16)) ** s).astype(np.int64), 63)
    fa[:, 1::2] = np.where(rng.random((1, 4, 1, 16)) < 0.5, 63 - u, u)
    ru = fa[rng.integers(0, N, (8, 16)), np.arange(8)[:, None], rng.integers(0, W, (8, 16))]
    cl = names(rng, rng.choice(np.array([M, M + M // 2, W // 2]), (8, 16, 1))); cl[:, 4:] = W - 1 - cl[:, 4:]
    return pack(fa, cl, ru)
def setup_inputs_ends(rng):
    h = M // 2; s = np.concatenate([np.arange(h), np.arange(W // 2 - h, W // 2)]); o = np.stack([rng.permutation(s) for g in range(8)])
    for g in (1, 3, 5, 7):
        j = int(np.argmax(o[g])); o[g, j] = o[g, M - 1]; o[g, M - 1] = W // 2 - 1
    pairs = o.reshape(8, N, K); cl = spots(rng, pairs, (1, 3, 5, 7)); cl[N - 1, 7, :, K - 1] = W - 1
    q = np.argsort(rng.random((N, 8, 16)), axis=-1) < 8; q[:, 2] = q[0, 2].copy(); q[:, 6] = q[0, 6].copy()
    n = rng.integers(0, 7, (N, 8, M)); n[:, 3] = rng.integers(1, 7, (N, M)); n[:, 7] = rng.integers(1, 7, (N, M))
    n[:, 3, M - 2:] = 0; n[:, 7, M - 1] = 0
    for g in (2, 6):
        for r in range(N - 1): n[r, g, r * K + int(rng.integers(0, K))] = 8
    flip = rows(rng, n); rec = 63 * (q[:, :, None] ^ flip).astype(np.int64)
    for g in (0, 1, 4, 5):
        for r in range(N):
            if g % 4 == 0:
                k = rng.integers(0, 4, h); k[0] = 0; a = swaps(rng, q[r, g], k)
            else:
                a = flip[r, g, :h].copy(); a[0] = False
            e = a[rng.permutation(h)]
            if g % 4 == 1: a, e = np.concatenate([a, a[:1]]), a[1:]
            t = np.concatenate([q[r, g] ^ a, ~q[r, g] ^ e]); v = 63 * t.astype(np.int64)
            if g % 4 == 0:
                u = rows(rng, rng.integers(0, 8, M)).astype(np.int64); u = u[:, :8] + u[:, 8:]; u[0] = 1; v[~t] = u.reshape(-1)
            rec[r, g] = np.concatenate([v[1:][rng.permutation(M - 1)], v[:1]])
    ru = np.stack([q[k % N] if k % 5 != 4 else ~q[0] for k in range(16)], axis=1)
    rest = 63 * (rng.random((N, 8, W // 2, 16)) < 0.5).astype(np.int64)
    return pack(lay(pairs, rec, rest), cl, 63 * ru.astype(np.int64))
def setup_inputs_corners(rng):
    o = np.stack([rng.permutation(M) for g in range(8)]); o[0] = np.arange(M); o[1] = np.arange(M)[::-1]
    o[1::2] += W // 2 - M; pairs = o.reshape(8, N, K); cl = spots(rng, pairs, ())
    bit = rng.integers(0, 2, (8, N, K)); bit[0] = 0; bit[1] = 1
    for g in (0, 1, 2, 3, 6, 7): cl[:, g] = (2 * pairs[g] + bit[g])[:, None]
    q = np.repeat(rng.choice(np.array([0, 1, 31, 32, 62, 63]), (1, 8, 16)), N, axis=0)
    q = np.where(rows(rng, np.full((N, 8), 2)), off(rng, q, 1, 4), q)
    x = np.repeat(q[:, :, None], W, axis=2); far = rng.integers(3, 6, (N, 8, W, 1)); eq = rng.integers(8, 11, (N, 8, W, 1))
    pos = np.argsort(rng.random(x.shape), axis=-1)
    x = np.where(pos < far, off(rng, x, 2, 3), np.where(pos < 16 - eq, off(rng, x, 1, 2), x))
    x = np.where(rng.random((N, 8, W, 1)) < 0.125, rng.integers(0, 64, x.shape), x)
    x[:, 4:] = np.where(rng.random((N, 4, W, 1)) < 0.03, q[:, 4:, None], x[:, 4:])
    for g, js in ((0, (0,)), (1, (M - 1,)), (2, (M - 2, M - 1)), (3, (K, M - 1))):
        for j in js: x[:, g, int(cl[:, g, 0].reshape(-1)[j])] = q[:, g]
    return pack(x, cl, np.stack([q[k % N] for k in range(16)], axis=1))
def camps(rng, q, n):
    pairs = np.stack([rng.permutation(W // 2)[:M] for g in range(8)]).reshape(8, N, K)
    far = rng.integers(0, 7, (N, 8, N, K)); u = np.argsort(rng.random((N, 8, K)), axis=-1)
    for r in range(N):
        far[r, :, r] = np.where(u[r] < n[:, r, None], 7, 8); far[r, :, (r + 1) % N, K - 1] = 0
    x = np.broadcast_to(q[None, :, None, None], (N, 8, N, K, 16)); rec = np.where(rows(rng, far), off(rng, x, 2, 8), x).reshape(N, 8, M, 16)
    y = np.broadcast_to(q[None, :, None], (N, 8, W // 2, 16)); rest = np.where(rows(rng, rng.integers(0, 7, (N, 8, W // 2))), off(rng, y, 2, 8), y)
    t = np.repeat(q[:, None], 16, axis=1); v = np.where(rows(rng, np.full((8, 16), 2)), off(rng, t, 1, 2), t)
    return lay(pairs, rec, rest), spots(rng, pairs, ()), np.where((np.arange(16) % 2 == 0)[None, :, None], t, v)
def setup_inputs_crowd(rng):
    n = K - rng.integers(0, 2, (8, N)); n[0] = K - 1; n[0, N - 1] = K; n[1] = K; n[2] = 0; n[3] = 0; n[3, 0] = K; n[7] = K; n[7, 0] = K - 1
    q = rng.integers(0, 4, (8, 16)); q[::2] += 60
    x, cl, ru = camps(rng, q, n)
    p = rng.permutation(np.setdiff1d(np.arange(W // 2), cl[:, 1] >> 1))[:M].reshape(N, K)
    cl[:, 1, 16 - N:] = (2 * p + rng.integers(0, 2, p.shape))[:, None]; ru[1, 16 - N:] = q[1]
    for r in range(N):
        far = rng.integers(0, 7, (N, K)); far[0] = rng.integers(0, 5, K); far[r] = 7; far[(r + 1) % N, K - 1] = 0
        v = mix(rng, q[1], far, 2, 8)
        if r == 0:
            u = np.argsort(rng.random((K, 16)), axis=-1); y = np.broadcast_to(q[1], (K, 16))
            v[0] = np.where(u < rng.integers(0, 5, (K, 1)), off(rng, y, 2, 8), np.where(u < 8, off(rng, y, 1, 2), y))
        put(x, r, 1, p, v)
    p = cl[:, 4, 0] >> 1
    for r in range(N):
        far = rng.integers(0, 5, (N, K)); far[(r + 1) % N, K - 1] = 0
        put(x, r, 4, p, mix(rng, q[4], far, 2, 8))
    p = cl[:, 5, 0] >> 1; s = rng.integers(0, 2, W // 2); cl[:, 5] = 2 * (cl[:, 5] >> 1) + s[cl[:, 5] >> 1]
    for r in range(N):
        far = rng.integers(5, 7, (N, K)); far[(r + 1) % N, K - 1] = 0; x[r, 5, 2 * p + s[p]] = mix(rng, q[5], far, 2, 8)
        far = rng.integers(1, 5, (N, K)); far[(r + 1) % N, K - 1] = 0; x[r, 5, 2 * p + 1 - s[p]] = mix(rng, q[5], far, 16, 32)
    p = (cl[:, 6, 0] >> 1).reshape(M); low = q[6] - rng.integers(8, 16, 16)
    for r in range(N):
        v = np.repeat(np.stack([q[6], low]), M // 2, axis=0)
        v = np.clip(v + rows(rng, np.full(M, 2)) * np.where(np.arange(M) < M // 2, 1, -1)[:, None], 0, 63)
        e = rng.permutation(16)[:(4, 12)[r % 2]]; v[rng.permutation(M // 2)[:e.size], e] = low[e]
        put(x, r, 6, p, v)
    return pack(x, cl, ru)
def setup_inputs_calm(rng):
    n = rng.integers(0, 4, (8, N))
    for g in (0, 2, 4, 6): n[g] = rng.permutation(N) % 4
    q = rng.integers(0, 4, (8, 16)); q[1::2] += 60
    return pack(*camps(rng, q, n))
def check_inputs(d):
    bad = []
    for k, lo, hi in (("fa", 0, 63), ("cl", 0, W - 1), ("ru", 0, 63)):
        v = np.asarray(d[k], np.float64)
        if not (np.min(v) >= lo and np.max(v) <= hi): bad.append("range of " + k)
        elif np.any(v != np.floor(v)): bad.append("whole numbers of " + k)
    v = np.asarray(d["ru"], np.float64)
    if np.any(v != v[:1]): bad.append("ru alike on all ranks")
    p = (np.asarray(d["cl"]).astype(np.int64) >> 1).reshape(N, 8, 16, K).transpose(1, 2, 0, 3).reshape(8, 16, M)
    p = np.sort(p, axis=-1)
    if np.any(p[..., 1:] == p[..., :-1]): bad.append("pairs of cl differ in a group and issue")
    return bad
def reference(fa, cl, ru):
    x = np.ascontiguousarray(np.asarray(fa, np.float32).astype(np.int64).reshape(N, 8, 16, W).transpose(0, 1, 3, 2))
    c = cl.astype(np.int64).reshape(N, 8, 16, K)
    b = np.asarray(ru[0], np.float32).astype(np.int64).reshape(8, 16, 16).transpose(0, 2, 1).copy()
    g8 = np.arange(8)[:, None]
    for rnd in range(RO):
        vote = np.zeros((N, 8, 16), np.int64)
        for r in range(N):
            z = x[r][g8[:, :, None], c[r]]
            eq = np.add.reduce((z == b[:, :, None]).astype(np.int64), axis=3)
            vote[r] = np.add.reduce((eq >= 9).astype(np.int64), axis=2)
        court = np.zeros((8, 16), np.int64)
        for g in range(8):
            taken = np.zeros(N, bool)
            for k in range(16):
                if k % N == 0: taken = np.zeros(N, bool)
                court[g, k] = np.argmax(np.where(taken, -1, vote[:, g, k])); taken[court[g, k]] = True
        up = np.zeros((N, 8, 16, K), bool)
        for k in range(16):
            r = court[:, k][:, None]; nm = c[:, :, k].transpose(1, 0, 2).reshape(8, M)
            z = x[r, g8, nm]
            med = np.sort(z, axis=1)[:, M // 2]
            dist = np.add.reduce(np.abs(z - med[:, None]), axis=2)
            b[:, k] = z[np.arange(8), np.argmin(dist, axis=1)]
            diff = b[:, k][:, None] - z
            ok = np.add.reduce((np.abs(diff) <= 1).astype(np.int64), axis=2) >= 12
            x[r, g8, nm] = z + np.where(ok[..., None], np.sign(diff), 0)
            up[:, :, k] = ok.reshape(8, N, K).transpose(1, 0, 2)
        c = np.where(up, c, c ^ 1)
    yb = np.ascontiguousarray(b.transpose(0, 2, 1)).reshape(128, 16).astype(np.float32).astype(BF)
    return {"yf": np.ascontiguousarray(x.transpose(0, 1, 3, 2)).reshape(N, 128, W).astype(np.float32).astype(BF), "yc": c.reshape(N, 128, K).astype(np.float32), "yr": np.stack([yb] * N)}

@@ -1,0 +1,586 @@
+from concourse.bass import DstId, RemoteDMATransfer
+from concourse.mybir import AluOpType as ALU, AxisListType as AX, ActivationFunctionType as ACT
+
+N, W, RO = 8, 6144, 4
+F, B, I, U = "float32", "bfloat16", "int32", "uint16"
+NSAT = 4
+
+
+def _scratch():
+    s = {}
+    for n, w, d in (
+        ("TB", 2 * W, B), ("CLS", 128, I), ("RU", 16, B), ("L0", 128, U), ("CLF", 1024, F), ("TMPF", 1024, F),
+        ("CL16", 1024, U), ("BI", 1024, I), ("PKI", 128, I), ("DUP", 256, F), ("TRN", 256, F), ("BL8", 128, B),
+        ("IP", 2, I), ("CI", 8, I), ("CF", 8, F), ("D", 16, F), ("IOD", 16, F), ("IN", 144, F), ("IG", 128, F),
+        ("IK", 128, F), ("IA", 128, F), ("IR", 128, F),
+        ("E16", 144, B), ("EZ", 144, B), ("EM", 144, B), ("EP", 144, B), ("BLK", 128, B), ("RN", 64, B), ("CN", 64, B),
+        ("CU", 128, B), ("MASKC", 32, F), ("CB", 16, F), ("SELB", 8, F), ("C8", 8, F), ("CY", 16, F),
+        ("SEL1", 64, F), ("SEL2", 64, F), ("HC", 128, B), ("MASK", 128, B), ("TA", 128, F), ("TC", 128, F),
+        ("OFFD", 16, U), ("OFF0", 8, U), ("OFFX", 8, U), ("OFFY", 8, U), ("OFFU", 8, U), ("OFFC", 16, U), ("OFFR", 2, U),
+        ("EQ", 2048, B), ("AB", 384, B), ("JK", 128, B), ("X", 128, B), ("RF", 16, F),
+        ("PEN", 128, F), ("CM", 8, F), ("MN", 16, F), ("RD", 8, F), ("OS", 8, U), ("L16", 128, U),
+        ("VV", 128, F), ("UI", 64, I), ("FF", 64, F), ("OO", 64, F),
+        ("OF", 64, U), ("SG", 128, B), ("HS", 128, B),
+        ("Z1", 1024, B), ("Z2", 1024, B), ("ZS", 1024, B), ("SJ", 1024, B), ("IND", 6192, B), ("SC", 1032, B), ("PW", 8, F),
+        ("RL", 1024, B), ("NS", 1024, B), ("MC", 16, F), ("SCOL", 32, F),
+        ("K1", 40, F), ("KD", 96, F), ("KE", 40, F), ("KJ", 2, U), ("KT", 96, F), ("KU", 40, F), ("BB", 16, F),
+        ("OFFL", 8, U),
+        ("NLF", 256, F), ("YC", 128, F), ("YR", 16, B),
+    ):
+        s[n] = ("sbuf", [128, w], d)
+    for n in ("NI", "NF", "T1", "SS"):
+        s[n] = ("sbuf", [128, 128], F)
+    s["ZO"] = ("sbuf", [128, 64, 16], B)
+    s["NE"] = ("sbuf", [128, 64, 16], B)
+    for n in range(RO):
+        s["NL%d" % n] = ("sbuf", [128, 256], U)
+        s["MSG%d" % n] = ("sbuf", [128, 16, 16], U)
+        s["VL%d" % n] = ("sbuf", [128, 32], F)
+        if n < RO - 1:
+            s["PKL%d" % n] = ("sbuf", [128, 128], B)
+    for n in ("KEY", "NR", "VC", "UU", "P20", "P21", "PV"):
+        s[n] = ("psum", [128, 512], F)
+    return s
+
+
+SCRATCH = _scratch()
+SEMAPHORES = (["sV", "sS", "sP", "sG", "loc", "ac", "hc", "dcl", "dru", "dfa", "dyf", "dyc", "dyr"]
+              + ["an%d_%d" % (n, b) for n in range(RO) for b in range(2)] + ["av%d" % n for n in range(RO)]
+              + [k + "%d" % n for k in ("ap", "hp") for n in range(RO - 1)])
+
+KNEAR = float(2 ** 24 + 4)
+MEVEN = 1.5 * 2 ** 24
+M1024 = 1.5 * 2 ** 33
+BIG, FAR = 4096.0, 1048576.0
+
+
+def _bits(cols):
+    m = 0
+    for c in cols:
+        m |= 1 << c
+    return m
+
+
+def _helper(T, topo, r):
+    c = T.cores[r]
+    ok = [h for h in topo.cores_of(c) if T.rank_of(h) is None and all(topo.may_write(h, d) for d in T.cores)]
+    return ([h for h in ok if topo.die(h) == topo.die(c)] + ok)[0]
+
+
+def _far(T, topo, c, ranks):
+    return [e for e in topo.engines(c, T.cores[ranks[0]]) if all(e in topo.engines(c, T.cores[r]) for r in ranks)]
+
+
+def _dst(topo, c):
+    rid, pid, _ = topo.addr(c)
+    return DstId(rid=rid, pnc=pid)
+
+
+def _copy_to(T, topo, cores, eng, sem, src, dst):
+    return RemoteDMATransfer(dst_ids=[_dst(topo, c) for c in cores], dma_engine_mask=_bits(eng), remote_sem=T.sem[sem],
+                             srcs=[src], dsts=[dst for c in cores])
+
+
+def _handed(r):
+    return [(r + d) % N for d in (5, 6, 7)]
+
+
+def _hand_on(g, core, T, topo, r):
+    peers = [p for p in range(N) if p != r]
+    eng = _far(T, topo, core, peers)
+    got = len(topo.engines(T.cores[r], core)) - len(_far(T, topo, T.cores[r], peers))
+    jobs = [("hc", "ac", T.L0[:], T.CL16[:, 128 * r:128 * r + 128], _handed(r))]
+    for n in range(RO - 1):
+        ap = T["PKL%d" % n][:, 16 * r:16 * r + 16]
+        jobs.append(("hp%d" % n, "ap%d" % n, ap, ap, peers))
+    for sem, out, src, dst, to in jobs:
+        g.wait_ge(T.sem[sem], got)
+        g.remote_dma_fused([_copy_to(T, topo, [T.cores[p] for p in to], eng, out, src, dst)], local_sem=T.sem.loc)
+    g.wait_ge(T.sem.loc, len(eng) * len(jobs))
+
+
+def _emit(g, T, ops):
+    queue = {"V": g.vector, "S": g.scalar, "P": g.tensor, "G": g, "Y": g.sync}
+    hist = {}
+    deps = []
+    target = set()
+    for i, o in enumerate(ops):
+        d = set()
+        for wr, regs in ((False, o["R"]), (True, o["W"])):
+            for n, m in regs:
+                ps = SCRATCH[n][0] == "psum"
+                for j, w2, m2 in hist.get(n, ()):
+                    same = ops[j]["q"] == o["q"]
+                    if ps and not same:
+                        d.add(j)
+                    elif m & m2 and (wr or w2) and not (same and o["q"] == "P"):
+                        d.add(j)
+        for wr, regs in ((False, o["R"]), (True, o["W"])):
+            for n, m in regs:
+                h = hist.setdefault(n, [])
+                if wr:
+                    h[:] = [e for e in h if e[2] & ~m]
+                h.append((i, wr, m))
+        best = {}
+        for j in d:
+            if ops[j]["tok"] is None:
+                best[ops[j]["q"]] = max(best.get(ops[j]["q"], -1), j)
+        d = set(best.values()) | set(j for j in d if ops[j]["tok"] is not None)
+        deps.append(d)
+        target |= d
+    last = {}
+    count = {}
+    known = {q: {} for q in queue}
+    token = {}
+    clock = {}
+    for i, o in enumerate(ops):
+        q = o["q"]
+        if q is None:
+            token[i] = o["tok"]
+            clock[i] = {o["tok"][0]: o["tok"][1]}
+            last[o["tok"][0]] = o["tok"][1]
+            continue
+        k = known[q]
+        for j in sorted(deps[i], reverse=True):
+            s, v = token[j]
+            if k.get(s, 0) < v:
+                queue[q].wait_ge(T.sem[s], v)
+                for s2, v2 in clock[j].items():
+                    k[s2] = max(k.get(s2, 0), v2)
+        ins = o["fn"]()
+        if o["tok"] is not None:
+            s, v = o["tok"]
+            if s != "loc":
+                ins.then_inc(T.sem[s], 16)
+        elif i in target:
+            s = "s" + q
+            count[s] = v = count.get(s, 0) + 1
+            ins.then_inc(T.sem[s], 1)
+        else:
+            continue
+        token[i] = (s, v)
+        clock[i] = dict(k)
+        clock[i][s] = v
+        last[s] = v
+    for s, v in last.items():
+        if max(k.get(s, 0) for k in known.values()) < v:
+            g.wait_ge(T.sem[s], v)
+
+
+def rank_program(g, core, T, topo):
+    me = T.rank_of(core)
+    if me is None:
+        for r in range(N):
+            if _helper(T, topo, r) == core:
+                _hand_on(g, core, T, topo, r)
+        return
+    ops = []
+    peers = [r for r in range(N) if r != me]
+    sent = [0]
+
+    def A(n, lo=None, hi=None, st=1):
+        if lo is None:
+            w = 1
+            for e in SCRATCH[n][1][1:]:
+                w *= e
+            return (T[n][:], [(n, (1 << w) - 1)], [])
+        if hi is None:
+            hi = lo + 1
+        ap = T[n][:, lo:hi] if st == 1 else T[n][:, lo:hi:st]
+        return (ap, [(n, _bits(range(lo, hi, st)))], [])
+
+    def A3(n, rows, cols):
+        h, w = SCRATCH[n][1][1:]
+        cs = [cols] if isinstance(cols, int) else range(w)[cols]
+        rs = [rows] if isinstance(rows, int) else range(h)[rows]
+        return (T[n][:, rows, cols], [(n, _bits(r * w + c for r in rs for c in cs))], [])
+
+    def GI(win, off):
+        return (win[0].indirect(off[0]), win[1], off[1])
+
+    def add(q, fn, outs, ins, tok=None):
+        rd, wr = [], []
+        for x in ins:
+            if isinstance(x, tuple):
+                rd += x[1] + x[2]
+        for x in outs:
+            wr += x[1]
+            rd += x[2]
+        ops.append({"q": q, "fn": fn, "R": rd, "W": wr, "tok": tok})
+
+    def P(x):
+        return x[0] if isinstance(x, tuple) else x
+
+    def ts(o, a, s1, op0, s2=None, op1=None):
+        if op1 is None:
+            add("V", lambda: g.vector.tensor_scalar(o[0], a[0], P(s1), None, op0), [o], [a, s1])
+        else:
+            add("V", lambda: g.vector.tensor_scalar(o[0], a[0], P(s1), P(s2), op0, op1), [o], [a, s1, s2])
+
+    def tt(o, a, b, op):
+        add("V", lambda: g.vector.tensor_tensor(o[0], a[0], b[0], op), [o], [a, b])
+
+    def cp(o, a):
+        add("V", lambda: g.vector.tensor_copy(o[0], a[0]), [o], [a])
+
+    def red(o, a, op, neg=False, ab=False):
+        add("V", lambda: g.vector.tensor_reduce(o[0], a[0], AX.X, op, negate=neg, apply_absolute_value=ab), [o], [a])
+
+    def scan(o, d0, d1, init, op0, op1):
+        add("V", lambda: g.vector.tensor_tensor_scan(o[0], d0[0], d1[0], P(init), op0, op1), [o], [d0, d1, init])
+
+    def tr(o, a):
+        add("V", lambda: g.vector.transpose(o[0], a[0]), [o], [a])
+
+    def ms(o, v):
+        add("V", lambda: g.vector.memset(o[0], v), [o], [])
+
+    def act(o, a, f, bias=0.0, scale=1.0, acc=None):
+        if acc is None:
+            add("S", lambda: g.scalar.activation(o[0], a[0], f, bias=P(bias), scale=scale), [o], [a, bias])
+        else:
+            add("S", lambda: g.scalar.activation(o[0], a[0], f, bias=P(bias), scale=scale, accum_out=acc[0]),
+                [o, acc], [a, bias])
+
+    def mm(o, l, r, start, stop):
+        add("P", lambda: g.tensor.matmul(o[0], l[0], r[0], start, stop), [o], [l, r])
+
+    def iota(o, pat, cm=0):
+        if SCRATCH[o[1][0][0]][2] == I:
+            add("G", lambda: g.iota(o[0], pat, 0, cm), [o], [])
+        else:
+            add("G", lambda: g.iota(o[0], pat, 0, cm, allow_small_or_imprecise_dtypes=True), [o], [])
+
+    def dma(q, o, a, sem):
+        e = g.sync if q == "Y" else g.scalar
+        add(q, lambda: e.dma_start(o[0], a[0]), [o], [a], (sem, 16))
+
+    def X(ap):
+        return (ap, [], [])
+
+    eng = _far(T, topo, core, peers)
+    helper = _helper(T, topo, me)
+    near = [e for e in topo.engines(core, helper) if e not in eng]
+
+    def send(src, parts):
+        sent[0] += sum(len(p[1]) for p in parts)
+        ts_ = [_copy_to(T, topo, cores, e, sem, src[0], to) for cores, e, sem, to in parts]
+        add("G", lambda: g.remote_dma_fused(ts_, local_sem=T.sem.loc), [], [src], ("loc", sent[0]))
+
+    def send_each(n, b):
+        sent[0] += len(peers)
+        w = 16 if n == RO - 1 else 10
+        src = [A3("MSG%d" % n, 2 * r + b, slice(0, w)) for r in peers]
+        c = 16 * (2 * me + b)
+        ts_ = [RemoteDMATransfer(dst_ids=[_dst(topo, T.cores[r])], dma_engine_mask=1 << eng[i],
+                                 remote_sem=T.sem["an%d_%d" % (n, b)], src=src[i][0], dst=T["NL%d" % n][:, c:c + w])
+               for i, r in enumerate(peers)]
+        add("G", lambda: g.remote_dma_fused(ts_, local_sem=T.sem.loc), [], src, ("loc", sent[0]))
+
+    def arrive(n, step, lo, w, sem, per):
+        ops.append({"q": None, "fn": None, "R": [],
+                    "W": [(n, _bits(range(r * step + lo, r * step + lo + w))) for r in peers],
+                    "tok": (sem, per * len(peers))})
+
+    def WQ(n, q):
+        return A(n, 15 - q, 143 - q)
+
+    mul, sub, eq_, plus = ALU.mult, ALU.subtract, ALU.is_equal, ALU.add
+    shr, band = ALU.logical_shift_right, ALU.bitwise_and
+    TBG = A("TB", 0, W)
+    allc, all64 = slice(0, 16), slice(0, 64)
+
+    dma("Y", A("CLS"), X(T.cl[:]), "dcl")
+    dma("S", A("RU"), X(T.ru[:]), "dru")
+    dma("Y", TBG, X(T.fa[:]), "dfa")
+    iota(A("IP", 0), [[0, 1]], 1)
+    iota(A("IOD"), [[16, 8], [0, 2]])
+    iota(A("IN"), [[1, 144]])
+    iota(A("IK"), [[1, 16], [0, 8]])
+    iota(A("IG"), [[1, 8], [0, 16]])
+    iota(A("IR"), [[0, 16], [1, 8]])
+    iota(A("IA"), [[0, 8], [1, 8], [0, 2]])
+    ms(A("CB", 0), 0.0)
+    ms(A("CB", 1), 64.0 - KNEAR)
+    ms(A("CB", 2, 16), 0.0)
+    for c, (sh, m) in enumerate(((4, 7), (0, 15), (4, 1), (3, 1), (0, 7), (0, 1), (1, 7), (3, 15))):
+        ts(A("CI", c), A("IP", 0), sh, shr, m, band)
+    ms(A("CN"), 23.0 / 2048)
+    cp(A("CF"), A("CI"))
+    pg, x, ga, xh, xl, xb, x2, p8 = [A("CF", c) for c in range(8)]
+    D = [A("D", c) for c in range(16)]
+    ms(A("PEN", 0, 128, 2), -BIG)
+    ts(A("OFFD"), A("IOD"), x, plus)
+    ts(D[8], xl, 32.0, mul, xh, plus)
+    ts(D[1], pg, 16.0, mul, 15.0, plus)
+    ts(D[0], ga, 16.0, mul, D[8], plus)
+    ms(A("PEN", 1, 128, 2), -FAR)
+    ts(A("OFF0"), A("IN", 0, 8), 2.0, mul, D[0], plus)
+    for n in range(RO):
+        ms(A("MSG%d" % n), 0)
+        ms(A("VL%d" % n, 4 * me, 4 * me + 4), 0.0)
+    cp(A("DUP"), GI(A("CLS"), A("OFFD")))
+    tr(A("TRN"), A("DUP"))
+    cp(A("L0"), GI(A("TRN"), A("OFF0")))
+    send(A("L0"), [([T.cores[r] for r in peers if r not in _handed(me)], eng, "ac", T.CL16[:, 128 * me:128 * me + 128]),
+                   ([helper], near, "hc", T.L0[:])])
+    ts(A("E16"), A("IN"), D[1], eq_, 1.0 / 16, mul)
+    ts(D[3], ga, 16.0, mul, x, plus)
+    ts(D[4], xh, 8.0, mul)
+    ts(D[5], xl, -1.0, plus)
+    ts(D[6], x, 64.0, mul)
+    ts(D[7], x2, 4.0, mul)
+    ts(D[10], xb, -1.0, plus, 1.0 / 16, mul)
+    ts(D[11], xb, -32.0, mul)
+    ts(D[13], xh, 16.0, mul)
+    ts(D[14], xh, 64.0, mul, xl, plus)
+    ts(A("MASK"), A("IG"), xl, eq_)
+    ts(A("BLK"), A("IG"), pg, eq_, -4.0, mul)
+    ts(A("BL8"), A("IK"), p8, eq_, -4.0, mul)
+    ts(A("CU"), A("IA"), D[10], mul, D[11], plus)
+    ts(A("OFFX"), A("IN", 0, 8), 0.0, mul, D[7], plus)
+    ts(A("TA", 0, 8), A("IN", 0, 8), 128.0, mul, D[14], plus)
+    ts(A("KT", 0, 32), A("IG", 0, 32), ga, ALU.not_equal, float(2 ** 22), mul)
+    ms(A("KEY", 64, 96), 2.0 ** 23)
+    ms(A("KD", 0, 64), 0.0)
+    ms(A("TC", 0, 6), 0.5)
+    ms(A("IND", 1028, 6192, 1032), 0.0)
+    ms(A("IND", 1030, 6192, 1032), 0.0)
+    scan(A("PW", 0, 6), A("TC", 0, 6), A("KD", 0, 6), 64.0, mul, plus)
+    for c, f in ((512, 2.0 ** -11), (513, 1.5 * 2 ** 23), (514, 0.5), (1029, -1.5 * 2 ** 23)):
+        ts(A("IND", c, 6192, 1032), A("PW", 0, 6), f, mul)
+    ms(A("KE", 0, 32), 0.0)
+    ms(A("KE", 32), -511.5)
+    ms(A("KE", 33), M1024)
+    ms(A("KE", 34), -M1024)
+    ms(A("KU", 32, 35), 4 * M1024)
+    ts(D[15], xh, 16.0, mul, xl, plus)
+    ts(D[12], xh, 16.0, mul, 8.0, plus)
+    ts(A("OFFL", 0, 4), A("IN", 0, 4), 32.0, mul, D[15], plus)
+    ts(D[2], D[12], xl, plus)
+    ts(A("OFFL", 4, 8), A("IN", 0, 4), 32.0, mul, D[2], plus)
+    ts(A("EZ"), A("IN"), D[1], eq_, 1024.0, mul)
+    ts(A("EM"), A("IN"), D[1], eq_, -2048.0, mul)
+    ts(A("EP"), A("IN"), D[1], eq_, 2048.0, mul)
+    ts(A("RN"), A("IN", 0, 64), -1.0 / 64, mul)
+    ts(A("SELB"), A("TA", 0, 8), 56.0, plus, 512.0, mul)
+    ts(A("MASKC"), A("KT", 0, 32), D[6], plus)
+    cp(A("KD", 64), A("MASKC", 0))
+    tt(A("KD", 65, 96), A("MASKC", 1, 32), A("MASKC", 0, 31), sub)
+    ts(A("C8"), A("IN", 0, 8), D[4], plus, 1.0 / 16, mul)
+    ts(A("CY"), A("IOD"), 1.0 / 16, mul, D[13], plus)
+    ts(A("OFFY"), A("IN", 0, 8), 32.0, mul, D[3], plus)
+    ts(A("SEL1"), A("IR", 0, 64), xl, eq_, 1.0 / BIG, mul)
+    ts(A("HC"), A("IR"), 0.0, ALU.is_gt, 2.0, mul)
+    ts(A("TC", 0, 64), A("IK", 0, 64), D[5], eq_, 1.0 / BIG, mul)
+    ts(A("TC", 64, 128), A("IK", 0, 64), xl, eq_, -1.0 / BIG, mul)
+    cp(A("CL16", 128 * me, 128 * me + 128), A("L0"))
+    tt(A("TA", 64, 128), A("TC", 0, 64), A("TC", 64, 128), plus)
+    tt(A("SEL2"), A("TA", 64, 128), A("IR", 0, 64), mul)
+    taken = A("PEN", 0, 128, 2)
+
+    def keep_own(n, b):
+        c = 16 * (2 * me + b)
+        cp(A("NL%d" % n, c, c + 16), A3("MSG%d" % n, 2 * me + b, allc))
+
+    for n in range(RO):
+        final = n == RO - 1
+        NL, MSG, pn = "NL%d" % n, "MSG%d" % n, "NL%d" % (n - 1)
+
+        def votes(b):
+            sl = list(range(8 * b, 8 * b + 8))
+            if n == 0:
+                names = {s: A("L0", 8 * s, 8 * s + 8) for s in sl}
+                rul = {s: A("RU", s) for s in sl}
+            else:
+                names = {8 * b + r: A(pn, 32 * r + 16 * b, 32 * r + 16 * b + 8) for r in range(N)}
+                rul = {s: A("RF", s) for s in sl}
+                arrive(pn, 32, 16 * b, 10, "an%d_%d" % (n - 1, b), 1)
+                cp(A("RF", 8 * b, 8 * b + 8), A(pn, 16 * b + 8, 256, 32))
+            e = [A("EQ", 1024 * b + 128 * i, 1024 * b + 128 * i + 128) for i in range(8)]
+            for i, s in enumerate(sl[5:]):
+                act(A("AB", 128 * i, 128 * i + 128), GI(TBG, names[s]), ACT.Abs, rul[s], -1.0)
+            act(A("EQ", 1024 * b + 640, 1024 * b + 896), A("AB", 0, 256), ACT.Sign)
+            act(e[7], A("AB", 256, 384), ACT.Sign)
+            for i in (0, 1, 2, 3, 5, 6, 7, 4):
+                if i < 5:
+                    ts(e[i], GI(TBG, names[sl[i]]), rul[sl[i]], ALU.not_equal)
+                mm(A("VC", 0, 128), WQ("E16", sl[i]), e[i], sl[i] == 0, sl[i] == 12)
+
+        VL = "VL%d" % n
+        mm(A("UU", 0, 128), A("BL8"), A("CU"), True, False)
+        votes(0)
+        if n > 0:
+            keep_own(n - 1, 1)
+        votes(1)
+        act(A("JK"), A("VC", 0, 128), ACT.Sign, 7.5 / 16, -1.0, A(VL, 4 * me))
+        src = A(VL, 4 * me, 4 * me + 4)
+        send(src, [([T.cores[r] for r in peers], eng, "av%d" % n, src[0])])
+        if n == 0:
+            arrive("CL16", 128, 0, 128, "ac", len(eng))
+            cp(A("CLF"), A("CL16"))
+            ts(A("TMPF"), A("CL16"), -0.5, plus, MEVEN, plus)
+            for h in range(2):
+                act(A("P2%d" % h), A("TMPF", 512 * h, 512 * h + 512), ACT.Identity, -MEVEN)
+        else:
+            pk = "PKL%d" % (n - 1)
+            tt(A("TA", 0, 64), taken, A("SEL2"), mul)
+            tt(A("TC", 0, 64), taken, A("SEL1"), mul)
+            red(A("RD", 2), A("TA", 0, 64), plus)
+            red(A("RD", 4), A("TC", 0, 64), plus)
+            ts(A("OFFU"), A("C8"), A("RD", 2), plus, 16.0, mul)
+            ts(A("MASK"), A("IG"), A("RD", 4), sub, 8.0, eq_)
+            arrive(pk, 16, 0, 16, "ap%d" % (n - 1), len(eng))
+            ts(A("PKI"), GI(A(pk), A("OFFU")), 255.0, plus, 0.5, mul)
+            for s in range(8):
+                ts(A("BI", s, 1024, 8), A("PKI"), 7 - s, shr, 1, band)
+            for h in range(2):
+                tt(A("CLF", 512 * h, 512 * h + 512), A("BI", 512 * h, 512 * h + 512), A("P2%d" % h), plus)
+        arrive(VL, 4, 0, 4, "av%d" % n, len(eng))
+        tt(A("X"), GI(A(VL), A("OFFX")), A("MASK"), mul)
+        mm(A("UU", 0, 128), A("BL8"), A("X"), False, True)
+        for i in range(7):
+            c = 16 * i
+            m = A("UU", c, c + 16, 2)
+            if i == 0:
+                red(A("MN", 15), m, ALU.min)
+            else:
+                scan(A("MN"), A("UU", c, c + 16), A("PEN", c - 16, c), FAR, sub, ALU.max)
+                tt(A("CM"), m, A("PEN", c - 16, c, 2), plus)
+                m = A("CM")
+            ts(A("PEN", c, c + 16, 2), m, A("MN", 15), ALU.is_le, -BIG, mul)
+        red(A("RD", 0), A("PEN", 2 * me, 112, 16), plus)
+        ts(A("OS"), A("SELB"), A("RD", 0), plus, 1.0 / 512, mul)
+        cp(A("NI"), GI(A("CLF"), A("OS")))
+        for b in range(2):
+            cp(A("L16", 64 * b, 64 * b + 64), GI(A("NI"), A("OFFL", 4 * b, 4 * b + 4)))
+
+        def H(k, b):
+            return A(k, 64 * b, 64 * b + 64)
+
+        def gather(zn, b):
+            act(A(zn, 512, 1024), GI(TBG, A("L16", 64 * b + 32, 64 * b + 64)), ACT.Identity)
+            cp(A(zn, 0, 512), GI(TBG, A("L16", 64 * b, 64 * b + 32)))
+
+        def key_open(zn):
+            mm(A("KEY", 0, 64), A("BLK"), A("RN"), True, False)
+            for q in range(16):
+                mm(A("KEY", 0, 64), WQ("EZ", q), A(zn, 64 * q, 64 * q + 64), False, False)
+            mm(A("NR", 0, 64), A("BLK"), A("CN"), True, False)
+
+        def sstep(i):
+            nb = -31.5 if i == 0 else A("SCOL", 15 + i)
+            act(A("SJ"), A("ZS"), ACT.Sign, nb, 1.0, A("SCOL", i))
+            act(A("SCOL", 8 + i), A("SCOL", i), ACT.Sign, 1.0)
+            act(A("SCOL", 16 + i), A("SCOL", 8 + i), ACT.Identity, nb, -16.0 / 2 ** i)
+
+        def lift(zn, lo, hi):
+            ts(A3("ZO", slice(lo, hi), allc), A(zn, 16 * lo, 16 * hi), 64.0, plus)
+
+        def half(h, i=0):
+            return A("IND", 1032 * i + 516 * h, 1032 * i + 516 * h + 512)
+
+        side = [lambda: cp(A("NF"), A("L16")),
+                lambda: ts(A("T1"), A("L16"), -0.5, plus, MEVEN, plus),
+                lambda: ts(H("PV", 0), H("T1", 0), -MEVEN, plus, 0.5, plus),
+                lambda: ts(H("PV", 1), H("T1", 1), -MEVEN, plus, 0.5, plus),
+                lambda: tt(H("SS", 0), H("NF", 0), H("PV", 0), sub),
+                lambda: tt(H("SS", 1), H("NF", 1), H("PV", 1), sub)]
+
+        gather("Z1", 0)
+        act(A("ZS"), GI(TBG, A("L16", 64, 128)), ACT.Identity)
+        key_open("Z1")
+        for i in range(NSAT):
+            sstep(i)
+        for i in range(6):
+            c, o = 1032 * i, 516 * (i % 2)
+            for h in range(2):
+                ts(half(h, i), A("Z1", 512 * h, 512 * h + 512), 32.0 if i == 0 else A("SC", 516 - o + 514), ALU.is_ge,
+                   2.0 ** (-5 - i), mul)
+            side[i]()
+            scan(A("SC", o, o + 515), A("IND", c, c + 515), A("IND", c + 516, c + 1031),
+                 0.0 if i == 0 else A("SC", 516 - o + 513), plus, plus)
+            lift("Z1", 8 * i, 8 * i + 8)
+
+        def hear(b, zn, med, nv, after_relu, after_sign):
+            cuts = [0, 4, 9, 13, 16] if nv == 16 else [0, 4, 8, nv]
+            for lo, hi in zip(cuts, cuts[1:]):
+                ts(A("RL", 64 * lo, 64 * hi), A(zn, 64 * lo, 64 * hi), med, sub, 0.0, ALU.min)
+            if nv < 16:
+                act(A("RL", 64 * nv, 1024), A(zn, 64 * nv, 1024), ACT.Relu, med, -1.0)
+            order = list(range(8)) + list(range(nv, 16)) + list(range(8, nv))
+            for q in order:
+                mm(A("KEY", 0, 64), WQ("EM" if q < nv else "EP", q), A("RL", 64 * q, 64 * q + 64), False, q == order[-1])
+            after_relu()
+            scan(A("KT"), A("KD"), A("KEY", 0, 96), 2.0 ** 23, plus, ALU.min)
+            tr(A("KU", 0, 32), A("KT", 64, 96))
+            scan(A("K1", 0, 35), A("KE", 0, 35), A("KU", 0, 35), 2.0 ** 23, plus, ALU.min)
+            ts(A("KJ", 0), A("K1", 31), A("K1", 34), sub)
+            tt(A("BB"), GI(A(zn), A("KJ", 0)), A("CB"), plus)
+            for lo, hi in ((0, 4), (4, 9), (9, 13), (13, 16)):
+                ts(A3("NE", all64, slice(lo, hi)), A3("ZO", all64, slice(lo, hi)), A("BB", 1), sub, KNEAR, eq_)
+            act(A("NS"), A(zn), ACT.Sign, A("BB", 0), -1.0)
+            for q in range(16):
+                mm(A("NR", 0, 64), WQ("E16", q), A3("NE", all64, q), False, q == 15)
+            cp(A3(MSG, slice(b, 16, 2), 8), A("BB", 2, 10))
+            f1 = lambda: ts(H("PV", 2), A("NR", 0, 64), 0.0, ALU.is_lt, float(W), mul)
+            vv = A("VV", 64 * b, 64 * b + 64)
+            f2 = lambda: tt(A("OO"), H("PV", 2), H("NF", b), plus)
+            f3 = lambda: cp(A("OF"), A("OO"))
+            v1 = lambda: tt(vv, A("NR", 0, 64), H("SS", b), mul)
+            v2 = lambda: tt(A("UI"), vv, H("PV", b), plus)
+            v3 = lambda: cp(A3(MSG, slice(b, 16, 2), slice(0, 8)), A("UI"))
+            sc = lambda: tt(GI(A("TB"), A("OF")), A(zn), A("NS"), plus)
+            for f in ((f1, v1, f2, v2, f3, v3) if b == 0 or final else (v1, f1, v2, f2, v3, f3)):
+                f()
+            send_each(n, b)
+            if not final:
+                act(H("SG", b), vv, ACT.Sign)
+            if b == 1 and not final:
+                pk = A("PKL%d" % n, 16 * me, 16 * me + 16)
+                scan(A("HS"), A("HC"), A("SG"), 0.0, mul, plus)
+                act(pk, A("HS", 7, 128, 8), ACT.Identity)
+                send(pk, [([helper], near, "hp%d" % n, pk[0])])
+            after_sign()
+            sc()
+
+        def s_finish():
+            for i in range(NSAT, 6):
+                sstep(i)
+            act(A("SCOL", 24), A("SCOL", 21), ACT.Identity, -0.5)
+            act(A("SCOL", 25), A("SCOL", 21), ACT.Identity, -1.0, -1.0)
+
+        hear(0, "Z1", A("SC", 516 + 513), 16, lambda: lift("Z1", 48, 64), s_finish)
+        gather("Z2", 1)
+        key_open("Z2")
+        for h in range(2):
+            ts(half(h), A("Z2", 512 * h, 512 * h + 512), A("SCOL", 25), ALU.is_gt)
+        keep_own(n, 0)
+        act(A("SJ"), A("Z2"), ACT.Sign, A("SCOL", 24), 1.0, A("SCOL", 26))
+        scan(A("SC", 0, 512), half(0), half(1), -511.5, plus, plus)
+        ts(A("MC", 6), A("SC", 511), 0.0, ALU.is_gt, A("SCOL", 25), plus)
+        ts(A("MC", 7), A("SCOL", 26), 0.0, ALU.is_ge, A("MC", 6), plus)
+
+        def lift2():
+            lift("Z2", 0, 32)
+            act(A3("ZO", slice(32, 64), allc), A("Z2", 512, 1024), ACT.Identity, 64.0)
+
+        hear(1, "Z2", A("MC", 7), 11, lift2, lambda: None)
+
+    dma("Y", X(T.yf[:]), TBG, "dyf")
+    keep_own(RO - 1, 1)
+    tt(A("TA", 0, 64), taken, A("SEL2"), mul)
+    red(A("RD", 2), A("TA", 0, 64), plus)
+    ts(A("RD", 7), A("RD", 2), 32.0, mul)
+    ts(A("OFFC"), A("CY"), A("RD", 7), plus)
+    ts(A("OFFR", 0), A("RD", 7), D[13], plus, 8.0, plus)
+    for b in range(2):
+        arrive("NL%d" % (RO - 1), 32, 16 * b, 16, "an%d_%d" % (RO - 1, b), 1)
+    cp(A("NLF"), A("NL%d" % (RO - 1)))
+    cp(A("DUP"), GI(A("NLF"), A("OFFC")))
+    cp(A("YR"), GI(A("NLF"), A("OFFR", 0)))
+    tr(A("TRN"), A("DUP"))
+    cp(A("YC"), GI(A("TRN"), A("OFFY")))
+    dma("S", X(T.yr[:]), A("YR"), "dyr")
+    dma("S", X(T.yc[:]), A("YC"), "dyc")
+    _emit(g, T, ops)

@@ -4,41 +4,42 @@ from concourse.mybir import AluOpType as ALU, AxisListType as AX, ActivationFunc
 N, W, RO = 8, 6144, 4
 F, B, I, U = "float32", "bfloat16", "int32", "uint16"
 NSAT = 4
+G2, G3, G4 = 5, 2, 4
+NVB = 11
+CUTS = [0, 2, 6, 11, 14, 16]
 
 
 def _scratch():
     s = {}
     for n, w, d in (
-        ("TB", 2 * W, B), ("CLS", 128, I), ("RU", 16, B), ("L0", 128, U), ("CLF", 1024, F), ("TMPF", 1024, F),
+        ("TB", W + 1024, B), ("CLS", 128, I), ("RU", 16, B), ("L0", 128, U), ("CLF", 1024, F), ("TMPF", 1024, F),
         ("CL16", 1024, U), ("BI", 1024, I), ("PKI", 128, I), ("DUP", 256, F), ("TRN", 256, F), ("BL8", 128, B),
         ("IP", 2, I), ("CI", 8, I), ("CF", 8, F), ("D", 16, F), ("IOD", 16, F), ("IN", 144, F), ("IG", 128, F),
-        ("IK", 128, F), ("IA", 128, F), ("IR", 128, F),
+        ("IK", 128, F), ("IR", 128, F),
         ("E16", 144, B), ("EZ", 144, B), ("EM", 144, B), ("EP", 144, B), ("BLK", 128, B), ("RN", 64, B), ("CN", 64, B),
         ("CU", 128, B), ("MASKC", 32, F), ("CB", 16, F), ("SELB", 8, F), ("C8", 8, F), ("CY", 16, F),
-        ("SEL1", 64, F), ("SEL2", 64, F), ("HC", 128, B), ("MASK", 128, B), ("TA", 128, F), ("TC", 128, F),
-        ("OFFD", 16, U), ("OFF0", 8, U), ("OFFX", 8, U), ("OFFY", 8, U), ("OFFU", 8, U), ("OFFC", 16, U), ("OFFR", 2, U),
-        ("EQ", 2048, B), ("AB", 384, B), ("JK", 128, B), ("X", 128, B), ("RF", 16, F),
-        ("PEN", 128, F), ("CM", 8, F), ("MN", 16, F), ("RD", 8, F), ("OS", 8, U), ("L16", 128, U),
-        ("VV", 128, F), ("UI", 64, I), ("FF", 64, F), ("OO", 64, F),
-        ("OF", 64, U), ("SG", 128, B), ("HS", 128, B),
-        ("Z1", 1024, B), ("Z2", 1024, B), ("ZS", 1024, B), ("SJ", 1024, B), ("IND", 6192, B), ("SC", 1032, B), ("PW", 8, F),
-        ("RL", 1024, B), ("NS", 1024, B), ("MC", 16, F), ("SCOL", 32, F),
+        ("SEL1", 8, F), ("ID", 1024, B), ("MASK", 16, F), ("VO", 4, F), ("MR", 128, F), ("RST", 128, F), ("PN", 256, F),
+        ("TA", 128, F), ("TC", 128, F),
+        ("OFFD", 16, U), ("OFF0", 8, U), ("OFFY", 8, U), ("OFFU", 8, U), ("OFFC", 16, U), ("OFFR", 2, U),
+        ("EQ", 2048, B), ("AB", 2048, B), ("JK", 128, B), ("RF", 16, F),
+        ("PEN", 128, F), ("CM", 64, F), ("MN", 16, F), ("RD", 8, F), ("OS", 8, U), ("L16", 128, U),
+        ("VV", 128, F), ("UI", 64, I), ("OO", 128, F),
+        ("OF", 64, U), ("SG", 128, B),
+        ("Z1", 1024, B), ("Z2", 1024, B), ("ZS", 1024, B), ("SJ", 1024, B), ("SS", 128, F), ("NI", 128, F), ("T1", 128, F), ("IB", 128, F),
+        ("OFFP", 16, U), ("DU2", 256, F), ("YQ", 16, B), ("SC", 1032, B), ("PW", 8, F),
+        ("RL", 1024, B), ("ZO", 1024, B), ("NE", 1024, B), ("NS", 1024, B), ("MC", 16, B), ("SCOL", 32, F),
         ("K1", 40, F), ("KD", 96, F), ("KE", 40, F), ("KJ", 2, U), ("KT", 96, F), ("KU", 40, F), ("BB", 16, F),
-        ("OFFL", 8, U),
         ("NLF", 256, F), ("YC", 128, F), ("YR", 16, B),
     ):
         s[n] = ("sbuf", [128, w], d)
-    for n in ("NI", "NF", "T1", "SS"):
-        s[n] = ("sbuf", [128, 128], F)
-    s["ZO"] = ("sbuf", [128, 64, 16], B)
-    s["NE"] = ("sbuf", [128, 64, 16], B)
+    s["IND"] = ("sbuf", [128, 12, 516], B)
     for n in range(RO):
         s["NL%d" % n] = ("sbuf", [128, 256], U)
         s["MSG%d" % n] = ("sbuf", [128, 16, 16], U)
-        s["VL%d" % n] = ("sbuf", [128, 32], F)
+        s["VL%d" % n] = ("sbuf", [128, 128], B)
         if n < RO - 1:
             s["PKL%d" % n] = ("sbuf", [128, 128], B)
-    for n in ("KEY", "NR", "VC", "UU", "P20", "P21", "PV"):
+    for n in ("KEY", "NR", "VC", "UU", "P20", "P21", "PV", "PP"):
         s[n] = ("psum", [128, 512], F)
     return s
 
@@ -50,8 +51,10 @@ SEMAPHORES = (["sV", "sS", "sP", "sG", "loc", "ac", "hc", "dcl", "dru", "dfa", "
 
 KNEAR = float(2 ** 24 + 4)
 MEVEN = 1.5 * 2 ** 24
+UNDER = 1.0 - 2.0 ** -14
 M1024 = 1.5 * 2 ** 33
 BIG, FAR = 4096.0, 1048576.0
+TINY = 2.0 ** -19
 
 
 def _bits(cols):
@@ -195,6 +198,9 @@ def rank_program(g, core, T, topo):
         rs = [rows] if isinstance(rows, int) else range(h)[rows]
         return (T[n][:, rows, cols], [(n, _bits(r * w + c for r in rs for c in cs))], [])
 
+    def top(n, p, w):
+        return (T[n][0:p, 0:w], [(n, (1 << w) - 1)], [])
+
     def GI(win, off):
         return (win[0].indirect(off[0]), win[1], off[1])
 
@@ -237,7 +243,7 @@ def rank_program(g, core, T, topo):
 
     def act(o, a, f, bias=0.0, scale=1.0, acc=None):
         if acc is None:
-            add("S", lambda: g.scalar.activation(o[0], a[0], f, bias=P(bias), scale=scale), [o], [a, bias])
+            add("S", lambda: g.scalar.activation(o[0], a[0], f, bias=P(bias), scale=P(scale)), [o], [a, bias, scale])
         else:
             add("S", lambda: g.scalar.activation(o[0], a[0], f, bias=P(bias), scale=scale, accum_out=acc[0]),
                 [o, acc], [a, bias])
@@ -296,29 +302,27 @@ def rank_program(g, core, T, topo):
     iota(A("IP", 0), [[0, 1]], 1)
     iota(A("IOD"), [[16, 8], [0, 2]])
     iota(A("IN"), [[1, 144]])
-    iota(A("IK"), [[1, 16], [0, 8]])
     iota(A("IG"), [[1, 8], [0, 16]])
     iota(A("IR"), [[0, 16], [1, 8]])
-    iota(A("IA"), [[0, 8], [1, 8], [0, 2]])
+    iota(A("IB"), [[2, 8], [0, 8], [1, 2]])
     ms(A("CB", 0), 0.0)
     ms(A("CB", 1), 64.0 - KNEAR)
     ms(A("CB", 2, 16), 0.0)
-    for c, (sh, m) in enumerate(((4, 7), (0, 15), (4, 1), (3, 1), (0, 7), (0, 1), (1, 7), (3, 15))):
+    for c, (sh, m) in enumerate(((4, 7), (0, 15), (4, 1), (3, 1), (0, 7), (0, 1), (1, 7), (1, 1))):
         ts(A("CI", c), A("IP", 0), sh, shr, m, band)
     ms(A("CN"), 23.0 / 2048)
     cp(A("CF"), A("CI"))
-    pg, x, ga, xh, xl, xb, x2, p8 = [A("CF", c) for c in range(8)]
+    pg, x, ga, xh, xl, xb, x2, xc = [A("CF", c) for c in range(8)]
     D = [A("D", c) for c in range(16)]
-    ms(A("PEN", 0, 128, 2), -BIG)
+    ms(A("PEN", 7, 128, 8), 0.0)
     ts(A("OFFD"), A("IOD"), x, plus)
-    ts(D[8], xl, 32.0, mul, xh, plus)
+    ts(D[8], xl, 4.0, mul, xh, plus)
     ts(D[1], pg, 16.0, mul, 15.0, plus)
-    ts(D[0], ga, 16.0, mul, D[8], plus)
-    ms(A("PEN", 1, 128, 2), -FAR)
-    ts(A("OFF0"), A("IN", 0, 8), 2.0, mul, D[0], plus)
+    ts(D[0], ga, 2.0, mul, D[8], plus)
+    ts(A("TA", 8, 16), A("IN", 0, 8), 1.0 / 8, mul)
+    ts(A("OFF0"), A("TA", 8, 16), D[0], plus, 8.0, mul)
     for n in range(RO):
         ms(A("MSG%d" % n), 0)
-        ms(A("VL%d" % n, 4 * me, 4 * me + 4), 0.0)
     cp(A("DUP"), GI(A("CLS"), A("OFFD")))
     tr(A("TRN"), A("DUP"))
     cp(A("L0"), GI(A("TRN"), A("OFF0")))
@@ -326,137 +330,155 @@ def rank_program(g, core, T, topo):
                    ([helper], near, "hc", T.L0[:])])
     ts(A("E16"), A("IN"), D[1], eq_, 1.0 / 16, mul)
     ts(D[3], ga, 16.0, mul, x, plus)
-    ts(D[4], xh, 8.0, mul)
-    ts(D[5], xl, -1.0, plus)
+    ts(D[4], xb, 8.0, mul)
+    ts(D[5], x2, -7.0, plus, BIG, mul)
     ts(D[6], x, 64.0, mul)
-    ts(D[7], x2, 4.0, mul)
-    ts(D[10], xb, -1.0, plus, 1.0 / 16, mul)
-    ts(D[11], xb, -32.0, mul)
-    ts(D[13], xh, 16.0, mul)
-    ts(D[14], xh, 64.0, mul, xl, plus)
-    ts(A("MASK"), A("IG"), xl, eq_)
+    ts(D[7], pg, 2.0, mul, xb, plus)
+    ts(D[10], xc, -1.0, plus, 1.0 / 16, mul)
+    ts(D[11], xc, -32.0, mul)
+    ts(D[13], xb, 16.0, mul)
+    ts(D[14], xb, 8.0, mul, x2, plus)
+    ts(D[2], xl, 2.0, mul, xh, plus)
+    ts(A("MASK"), A("IR", 0, 16), x2, eq_)
     ts(A("BLK"), A("IG"), pg, eq_, -4.0, mul)
-    ts(A("BL8"), A("IK"), p8, eq_, -4.0, mul)
-    ts(A("CU"), A("IA"), D[10], mul, D[11], plus)
-    ts(A("OFFX"), A("IN", 0, 8), 0.0, mul, D[7], plus)
+    ts(A("BL8"), A("IB"), D[7], eq_, -4.0, mul)
+    ts(A("OFFP"), A("IN", 0, 16), 16.0, mul, D[2], plus)
+    ts(A("CU"), A("IG"), D[10], mul, D[11], plus)
     ts(A("TA", 0, 8), A("IN", 0, 8), 128.0, mul, D[14], plus)
     ts(A("KT", 0, 32), A("IG", 0, 32), ga, ALU.not_equal, float(2 ** 22), mul)
     ms(A("KEY", 64, 96), 2.0 ** 23)
     ms(A("KD", 0, 64), 0.0)
     ms(A("TC", 0, 6), 0.5)
-    ms(A("IND", 1028, 6192, 1032), 0.0)
-    ms(A("IND", 1030, 6192, 1032), 0.0)
+    ms(A3("IND", slice(1, 12, 2), 512), 0.0)
+    ms(A3("IND", slice(1, 12, 2), 514), 0.0)
     scan(A("PW", 0, 6), A("TC", 0, 6), A("KD", 0, 6), 64.0, mul, plus)
-    for c, f in ((512, 2.0 ** -11), (513, 1.5 * 2 ** 23), (514, 0.5), (1029, -1.5 * 2 ** 23)):
-        ts(A("IND", c, 6192, 1032), A("PW", 0, 6), f, mul)
+    for h, c, f in ((0, 512, 2.0 ** -11), (0, 513, 1.5 * 2 ** 23), (0, 514, 0.5), (1, 513, -1.5 * 2 ** 23)):
+        ts(A3("IND", slice(h, 12, 2), c), A("PW", 0, 6), f, mul)
     ms(A("KE", 0, 32), 0.0)
     ms(A("KE", 32), -511.5)
     ms(A("KE", 33), M1024)
     ms(A("KE", 34), -M1024)
     ms(A("KU", 32, 35), 4 * M1024)
-    ts(D[15], xh, 16.0, mul, xl, plus)
-    ts(D[12], xh, 16.0, mul, 8.0, plus)
-    ts(A("OFFL", 0, 4), A("IN", 0, 4), 32.0, mul, D[15], plus)
-    ts(D[2], D[12], xl, plus)
-    ts(A("OFFL", 4, 8), A("IN", 0, 4), 32.0, mul, D[2], plus)
     ts(A("EZ"), A("IN"), D[1], eq_, 1024.0, mul)
     ts(A("EM"), A("IN"), D[1], eq_, -2048.0, mul)
     ts(A("EP"), A("IN"), D[1], eq_, 2048.0, mul)
     ts(A("RN"), A("IN", 0, 64), -1.0 / 64, mul)
-    ts(A("SELB"), A("TA", 0, 8), 56.0, plus, 512.0, mul)
+    ts(A("SELB"), A("TA", 0, 8), 112.0, plus, 256.0, mul)
     ts(A("MASKC"), A("KT", 0, 32), D[6], plus)
     cp(A("KD", 64), A("MASKC", 0))
     tt(A("KD", 65, 96), A("MASKC", 1, 32), A("MASKC", 0, 31), sub)
     ts(A("C8"), A("IN", 0, 8), D[4], plus, 1.0 / 16, mul)
     ts(A("CY"), A("IOD"), 1.0 / 16, mul, D[13], plus)
     ts(A("OFFY"), A("IN", 0, 8), 32.0, mul, D[3], plus)
-    ts(A("SEL1"), A("IR", 0, 64), xl, eq_, 1.0 / BIG, mul)
-    ts(A("HC"), A("IR"), 0.0, ALU.is_gt, 2.0, mul)
-    ts(A("TC", 0, 64), A("IK", 0, 64), D[5], eq_, 1.0 / BIG, mul)
-    ts(A("TC", 64, 128), A("IK", 0, 64), xl, eq_, -1.0 / BIG, mul)
+    ts(A("SEL1"), A("IN", 0, 8), x2, eq_, 1.0 / BIG, mul)
+    ts(D[9], pg, 16.0, mul, x, plus)
+    for s in range(8):
+        ts(A("ID", 128 * s, 128 * s + 128), A("IN", 0, 128), D[9], eq_, 2.0 ** (7 - s), mul)
+    ts(A("RST"), A("IR"), 0.0, ALU.is_gt, -FAR, mul)
     cp(A("CL16", 128 * me, 128 * me + 128), A("L0"))
-    tt(A("TA", 64, 128), A("TC", 0, 64), A("TC", 64, 128), plus)
-    tt(A("SEL2"), A("TA", 64, 128), A("IR", 0, 64), mul)
-    taken = A("PEN", 0, 128, 2)
+    ms(A("PN", 0, 256, 2), -1.0)
+    ts(A("NR", 1, 128, 2), A("IN", 0, 64), D[6], plus, -TINY, mul)
+    ts(A("NR", 1, 128, 2), A("NR", 1, 128, 2), -TINY * W, plus)
 
     def keep_own(n, b):
         c = 16 * (2 * me + b)
         cp(A("NL%d" % n, c, c + 16), A3("MSG%d" % n, 2 * me + b, allc))
 
+    def rulings(n, b):
+        arrive("NL%d" % n, 32, 16 * b, 10, "an%d_%d" % (n, b), 1)
+        cp(A("RF", 8 * b, 8 * b + 8), A("NL%d" % n, 16 * b + 8, 256, 32))
+
+    heard = A("MR", 7, 128, 16)
+
     for n in range(RO):
         final = n == RO - 1
         NL, MSG, pn = "NL%d" % n, "MSG%d" % n, "NL%d" % (n - 1)
 
-        def votes(b):
-            sl = list(range(8 * b, 8 * b + 8))
-            if n == 0:
-                names = {s: A("L0", 8 * s, 8 * s + 8) for s in sl}
-                rul = {s: A("RU", s) for s in sl}
-            else:
-                names = {8 * b + r: A(pn, 32 * r + 16 * b, 32 * r + 16 * b + 8) for r in range(N)}
-                rul = {s: A("RF", s) for s in sl}
-                arrive(pn, 32, 16 * b, 10, "an%d_%d" % (n - 1, b), 1)
-                cp(A("RF", 8 * b, 8 * b + 8), A(pn, 16 * b + 8, 256, 32))
-            e = [A("EQ", 1024 * b + 128 * i, 1024 * b + 128 * i + 128) for i in range(8)]
-            for i, s in enumerate(sl[5:]):
-                act(A("AB", 128 * i, 128 * i + 128), GI(TBG, names[s]), ACT.Abs, rul[s], -1.0)
-            act(A("EQ", 1024 * b + 640, 1024 * b + 896), A("AB", 0, 256), ACT.Sign)
-            act(e[7], A("AB", 256, 384), ACT.Sign)
-            for i in (0, 1, 2, 3, 5, 6, 7, 4):
-                if i < 5:
-                    ts(e[i], GI(TBG, names[sl[i]]), rul[sl[i]], ALU.not_equal)
-                mm(A("VC", 0, 128), WQ("E16", sl[i]), e[i], sl[i] == 0, sl[i] == 12)
+        slot = list(range(8)) + [8 + me] + [8 + r for r in peers]
+
+        def names(s):
+            c = 16 * (slot[s] % 8) + 8 * (slot[s] // 8)
+            return A("L0", c, c + 8) if n == 0 else A(pn, 2 * c, 2 * c + 8)
+
+        def rul(s):
+            return A("RU", slot[s]) if n == 0 else A("BB", 0) if s == 8 else A("RF", slot[s])
+
+        def count(lo, hi):
+            for s in range(lo, hi):
+                mm(A("VC", 0, 128), WQ("E16", 2 * (slot[s] % 8) + slot[s] // 8), A("EQ", 128 * s, 128 * s + 128),
+                   s == 0, s == 15)
+
+        def vgather(s):
+            ts(A("EQ", 128 * s, 128 * s + 128), GI(TBG, names(s)), rul(s), ALU.not_equal)
+            count(s, s + 1)
+
+        def sgather(lo, hi):
+            for s in range(lo, hi):
+                act(A("AB", 128 * s, 128 * s + 128), GI(TBG, names(s)), ACT.Abs, rul(s), -1.0)
+
+        def cut(lo, hi):
+            ts(A("EQ", 128 * lo, 128 * hi), A("AB", 128 * lo, 128 * hi), 1.0, ALU.min)
+            count(lo, hi)
 
         VL = "VL%d" % n
         mm(A("UU", 0, 128), A("BL8"), A("CU"), True, False)
-        votes(0)
         if n > 0:
             keep_own(n - 1, 1)
-        votes(1)
-        act(A("JK"), A("VC", 0, 128), ACT.Sign, 7.5 / 16, -1.0, A(VL, 4 * me))
-        src = A(VL, 4 * me, 4 * me + 4)
+        sgather(3, 8)
+        for s in (0, 1, 2, 8):
+            vgather(s)
+        cut(3, 6)
+        if n > 0:
+            rulings(n - 1, 1)
+        sgather(13, 16)
+        cut(6, 8)
+        for s in (9, 10, 11):
+            vgather(s)
+        cut(13, 15)
+        vgather(12)
+        cut(15, 16)
+        act(A("JK"), A("VC", 0, 128), ACT.Sign, 7.5 / 16, -1.0, A("VO", 0))
+        src = A(VL, 16 * me, 16 * me + 16)
+        act(src, A("MASK"), ACT.Identity, 0.0, A("VO", 0))
         send(src, [([T.cores[r] for r in peers], eng, "av%d" % n, src[0])])
         if n == 0:
             arrive("CL16", 128, 0, 128, "ac", len(eng))
             cp(A("CLF"), A("CL16"))
-            ts(A("TMPF"), A("CL16"), -0.5, plus, MEVEN, plus)
-            for h in range(2):
-                act(A("P2%d" % h), A("TMPF", 512 * h, 512 * h + 512), ACT.Identity, -MEVEN)
         else:
             pk = "PKL%d" % (n - 1)
-            tt(A("TA", 0, 64), taken, A("SEL2"), mul)
-            tt(A("TC", 0, 64), taken, A("SEL1"), mul)
-            red(A("RD", 2), A("TA", 0, 64), plus)
-            red(A("RD", 4), A("TC", 0, 64), plus)
-            ts(A("OFFU"), A("C8"), A("RD", 2), plus, 16.0, mul)
-            ts(A("MASK"), A("IG"), A("RD", 4), sub, 8.0, eq_)
             arrive(pk, 16, 0, 16, "ap%d" % (n - 1), len(eng))
             ts(A("PKI"), GI(A(pk), A("OFFU")), 255.0, plus, 0.5, mul)
             for s in range(8):
                 ts(A("BI", s, 1024, 8), A("PKI"), 7 - s, shr, 1, band)
             for h in range(2):
                 tt(A("CLF", 512 * h, 512 * h + 512), A("BI", 512 * h, 512 * h + 512), A("P2%d" % h), plus)
-        arrive(VL, 4, 0, 4, "av%d" % n, len(eng))
-        tt(A("X"), GI(A(VL), A("OFFX")), A("MASK"), mul)
-        mm(A("UU", 0, 128), A("BL8"), A("X"), False, True)
+        arrive(VL, 16, 0, 16, "av%d" % n, len(eng))
+        mm(A("UU", 0, 128), A("BL8"), A(VL), False, True)
         for i in range(7):
-            c = 16 * i
-            m = A("UU", c, c + 16, 2)
+            key, pen = [lambda j: A("UU", j, 128, 8), lambda j: A("PEN", j, 128, 8)]
+            high, down = [lambda j: key(j) if j < 2 else A("CM", 32 * (j % 2), 32 * (j % 2) + 16),
+                        lambda j: key(j) if j < 2 else A("CM", 32 * (j % 2) + 16, 32 * (j % 2) + 32)]
             if i == 0:
-                red(A("MN", 15), m, ALU.min)
+                red(A("MN", 15), A("UU", 0, 128, 16), ALU.min)
             else:
-                scan(A("MN"), A("UU", c, c + 16), A("PEN", c - 16, c), FAR, sub, ALU.max)
-                tt(A("CM"), m, A("PEN", c - 16, c, 2), plus)
-                m = A("CM")
-            ts(A("PEN", c, c + 16, 2), m, A("MN", 15), ALU.is_le, -BIG, mul)
-        red(A("RD", 0), A("PEN", 2 * me, 112, 16), plus)
-        ts(A("OS"), A("SELB"), A("RD", 0), plus, 1.0 / 512, mul)
+                scan(A("MN"), high(i), pen(i - 1), FAR, sub, ALU.max)
+            if 1 <= i <= 5:
+                tt(high(i + 1), key(i + 1), pen(i - 1), sub)
+            ts(pen(i), down(i), A("MN", 15), ALU.is_le, -BIG * (7 - i), mul)
+            if 1 <= i <= 5:
+                tt(down(i + 1), key(i + 1), pen(i - 1), plus)
+        red(A("RD", 0), A("PEN", 16 * me, 16 * me + 8), ALU.min)
+        ts(A("OS"), A("SELB"), A("RD", 0), plus, 1.0 / 256, mul)
         cp(A("NI"), GI(A("CLF"), A("OS")))
-        for b in range(2):
-            cp(A("L16", 64 * b, 64 * b + 64), GI(A("NI"), A("OFFL", 4 * b, 4 * b + 4)))
 
         def H(k, b):
             return A(k, 64 * b, 64 * b + 64)
+
+        def NH(k, b):
+            return A(k, b, 128, 2)
+
+        for b in range(2):
+            cp(H("L16", b), NH("NI", b))
 
         def gather(zn, b):
             act(A(zn, 512, 1024), GI(TBG, A("L16", 64 * b + 32, 64 * b + 64)), ACT.Identity)
@@ -466,7 +488,7 @@ def rank_program(g, core, T, topo):
             mm(A("KEY", 0, 64), A("BLK"), A("RN"), True, False)
             for q in range(16):
                 mm(A("KEY", 0, 64), WQ("EZ", q), A(zn, 64 * q, 64 * q + 64), False, False)
-            mm(A("NR", 0, 64), A("BLK"), A("CN"), True, False)
+            mm(A("NR", 0, 128, 2), A("BLK"), A("CN"), True, False)
 
         def sstep(i):
             nb = -31.5 if i == 0 else A("SCOL", 15 + i)
@@ -475,35 +497,53 @@ def rank_program(g, core, T, topo):
             act(A("SCOL", 16 + i), A("SCOL", 8 + i), ACT.Identity, nb, -16.0 / 2 ** i)
 
         def lift(zn, lo, hi):
-            ts(A3("ZO", slice(lo, hi), allc), A(zn, 16 * lo, 16 * hi), 64.0, plus)
+            ts(A("ZO", 16 * lo, 16 * hi), A(zn, 16 * lo, 16 * hi), 64.0, plus)
 
-        def half(h, i=0):
-            return A("IND", 1032 * i + 516 * h, 1032 * i + 516 * h + 512)
+        def half(h, i=0, w=512):
+            return A3("IND", 2 * i + h, slice(0, w))
 
-        side = [lambda: cp(A("NF"), A("L16")),
-                lambda: ts(A("T1"), A("L16"), -0.5, plus, MEVEN, plus),
-                lambda: ts(H("PV", 0), H("T1", 0), -MEVEN, plus, 0.5, plus),
-                lambda: ts(H("PV", 1), H("T1", 1), -MEVEN, plus, 0.5, plus),
-                lambda: tt(H("SS", 0), H("NF", 0), H("PV", 0), sub),
-                lambda: tt(H("SS", 1), H("NF", 1), H("PV", 1), sub)]
+        def slift(zn, lo, hi):
+            act(A("ZO", 16 * lo, 16 * hi), A(zn, 16 * lo, 16 * hi), ACT.Identity, 64.0)
 
+        side = [[lambda b=b: ts(H("PV", b), NH("T1", b), -MEVEN, plus, 0.5, plus),
+                 lambda b=b: ts(A("PN", 128 * b + 1, 128 * b + 128, 2), NH("NI", b), -TINY, mul),
+                 lambda b=b: tt(H("SS", b), NH("NI", b), H("PV", b), sub)] for b in range(2)]
+        lifts = [lambda i=i: lift("Z1", 8 * i, 8 * i + 8) for i in range(8)]
+        slots = [lambda: scan(A("MR"), A("RST"), A("PEN"), 0.0, ALU.max, ALU.min),
+                 lambda: tt(A("TC", 0, 8), heard, A("SEL1"), mul),
+                 lambda: ts(A("TA", 0, 8), heard, D[5], eq_),
+                 lambda: red(A("RD", 4), A("TC", 0, 8), plus),
+                 lambda: tt(A("TA", 8, 16), A("TA", 0, 8), A("IN", 0, 8), mul),
+                 lambda: ts(A("MASK"), A("IR", 0, 16), A("RD", 4), sub, 7.0, eq_),
+                 lambda: red(A("RD", 2), A("TA", 8, 16), plus),
+                 lambda: ts(A("OFFU"), A("C8"), A("RD", 2), plus, 16.0, mul)]
+
+        later = [side[0][0], side[1][0], side[0][1], side[0][2], side[1][2], side[1][1]] + slots
+
+        def gap(k=1):
+            for f in later[:k]:
+                f()
+            del later[:k]
+
+        act(A("T1"), A("NI"), ACT.Identity, MEVEN, UNDER)
         gather("Z1", 0)
         act(A("ZS"), GI(TBG, A("L16", 64, 128)), ACT.Identity)
         key_open("Z1")
         for i in range(NSAT):
             sstep(i)
         for i in range(6):
-            c, o = 1032 * i, 516 * (i % 2)
-            for h in range(2):
-                ts(half(h, i), A("Z1", 512 * h, 512 * h + 512), 32.0 if i == 0 else A("SC", 516 - o + 514), ALU.is_ge,
+            o = 516 * (i % 2)
+            if i == 0:
+                for h in range(2):
+                    ts(half(h), A("Z1", 512 * h, 512 * h + 512), 32.0, ALU.is_ge, 2.0 ** -5, mul)
+            else:
+                ts(A3("IND", slice(2 * i, 2 * i + 2), slice(0, 512)), A("Z1"), A("SC", 516 - o + 514), ALU.is_ge,
                    2.0 ** (-5 - i), mul)
-            side[i]()
-            scan(A("SC", o, o + 515), A("IND", c, c + 515), A("IND", c + 516, c + 1031),
+            scan(A("SC", o, o + 515), half(0, i, 515), half(1, i, 515),
                  0.0 if i == 0 else A("SC", 516 - o + 513), plus, plus)
-            lift("Z1", 8 * i, 8 * i + 8)
 
         def hear(b, zn, med, nv, after_relu, after_sign):
-            cuts = [0, 4, 9, 13, 16] if nv == 16 else [0, 4, 8, nv]
+            cuts = CUTS if nv == 16 else [0, 2, 5, 8, nv]
             for lo, hi in zip(cuts, cuts[1:]):
                 ts(A("RL", 64 * lo, 64 * hi), A(zn, 64 * lo, 64 * hi), med, sub, 0.0, ALU.min)
             if nv < 16:
@@ -517,29 +557,33 @@ def rank_program(g, core, T, topo):
             scan(A("K1", 0, 35), A("KE", 0, 35), A("KU", 0, 35), 2.0 ** 23, plus, ALU.min)
             ts(A("KJ", 0), A("K1", 31), A("K1", 34), sub)
             tt(A("BB"), GI(A(zn), A("KJ", 0)), A("CB"), plus)
-            for lo, hi in ((0, 4), (4, 9), (9, 13), (13, 16)):
-                ts(A3("NE", all64, slice(lo, hi)), A3("ZO", all64, slice(lo, hi)), A("BB", 1), sub, KNEAR, eq_)
+            parts = ((0, 8), (1, 4), (2, 4), (3, 4), (4, 8))
+            for c, st in parts:
+                ts(A("NE", c, 1024, st), A("ZO", c, 1024, st), A("BB", 1), sub, KNEAR, eq_)
             act(A("NS"), A(zn), ACT.Sign, A("BB", 0), -1.0)
-            for q in range(16):
-                mm(A("NR", 0, 64), WQ("E16", q), A3("NE", all64, q), False, q == 15)
+            order = [q for c, st in parts for q in range(c, 16, st)]
+            for q in order:
+                mm(A("NR", 0, 128, 2), WQ("E16", q), A("NE", q, 1024, 16), False, q == order[-1])
             cp(A3(MSG, slice(b, 16, 2), 8), A("BB", 2, 10))
-            f1 = lambda: ts(H("PV", 2), A("NR", 0, 64), 0.0, ALU.is_lt, float(W), mul)
+            if b == 1 and not final:
+                rulings(n, 0)
+            gap(G2 if b == 0 else 9)
             vv = A("VV", 64 * b, 64 * b + 64)
-            f2 = lambda: tt(A("OO"), H("PV", 2), H("NF", b), plus)
-            f3 = lambda: cp(A("OF"), A("OO"))
-            v1 = lambda: tt(vv, A("NR", 0, 64), H("SS", b), mul)
+            f1 = lambda: scan(A("OO"), A("PN", 128 * b, 128 * b + 128), A("NR", 0, 128), 0.0, ALU.min, ALU.max)
+            f2 = lambda: ts(A("OF"), A("OO", 1, 128, 2), -1.0 / TINY, mul)
+            v1 = lambda: tt(vv, A("NR", 0, 128, 2), H("SS", b), mul)
             v2 = lambda: tt(A("UI"), vv, H("PV", b), plus)
             v3 = lambda: cp(A3(MSG, slice(b, 16, 2), slice(0, 8)), A("UI"))
             sc = lambda: tt(GI(A("TB"), A("OF")), A(zn), A("NS"), plus)
-            for f in ((f1, v1, f2, v2, f3, v3) if b == 0 or final else (v1, f1, v2, f2, v3, f3)):
+            for f in (v1, f1, v2, f2, v3):
                 f()
             send_each(n, b)
-            if not final:
-                act(H("SG", b), vv, ACT.Sign)
             if b == 1 and not final:
+                act(H("SG", b), vv, ACT.Sign)
                 pk = A("PKL%d" % n, 16 * me, 16 * me + 16)
-                scan(A("HS"), A("HC"), A("SG"), 0.0, mul, plus)
-                act(pk, A("HS", 7, 128, 8), ACT.Identity)
+                for s in range(8):
+                    mm(A("PP", 0, 16), A("ID", 128 * s, 128 * s + 128), A("SG", s, 128, 8), s == 0, s == 7)
+                act(pk, A("PP", 0, 16), ACT.Identity)
                 send(pk, [([helper], near, "hp%d" % n, pk[0])])
             after_sign()
             sc()
@@ -547,38 +591,48 @@ def rank_program(g, core, T, topo):
         def s_finish():
             for i in range(NSAT, 6):
                 sstep(i)
+            act(A("MC", 0), A("SCOL", 21), ACT.Identity, -1.0, -1.0)
             act(A("SCOL", 24), A("SCOL", 21), ACT.Identity, -0.5)
-            act(A("SCOL", 25), A("SCOL", 21), ACT.Identity, -1.0, -1.0)
+            if not final:
+                act(H("SG", 0), H("VV", 0), ACT.Sign)
 
-        hear(0, "Z1", A("SC", 516 + 513), 16, lambda: lift("Z1", 48, 64), s_finish)
+        hear(0, "Z1", A("SC", 516 + 513), 16, lambda: lift("Z1", 0, 64), s_finish)
         gather("Z2", 1)
         key_open("Z2")
         for h in range(2):
-            ts(half(h), A("Z2", 512 * h, 512 * h + 512), A("SCOL", 25), ALU.is_gt)
+            ts(half(h, 5), A("Z2", 512 * h, 512 * h + 512), A("MC", 0), ALU.is_gt, 2.0 ** -10, mul)
         keep_own(n, 0)
         act(A("SJ"), A("Z2"), ACT.Sign, A("SCOL", 24), 1.0, A("SCOL", 26))
-        scan(A("SC", 0, 512), half(0), half(1), -511.5, plus, plus)
-        ts(A("MC", 6), A("SC", 511), 0.0, ALU.is_gt, A("SCOL", 25), plus)
-        ts(A("MC", 7), A("SCOL", 26), 0.0, ALU.is_ge, A("MC", 6), plus)
+        scan(A("SC", 0, 515), half(0, 5, 515), half(1, 5, 515), A("MC", 0), plus, plus)
+        gap(G3)
+        ts(A("MC", 7), A("SCOL", 26), 0.0, ALU.is_ge, A("SC", 513), plus)
 
-        def lift2():
-            lift("Z2", 0, 32)
-            act(A3("ZO", slice(32, 64), allc), A("Z2", 512, 1024), ACT.Identity, 64.0)
+        def after_relu2():
+            lift("Z2", 0, 24)
+            slift("Z2", 24, 64)
+            gap(G4)
 
-        hear(1, "Z2", A("MC", 7), 11, lift2, lambda: None)
+        def evens():
+            if n == 0:
+                act(A("TMPF"), A("CLF"), ACT.Identity, MEVEN, UNDER)
+                for h in range(2):
+                    act(A("P2%d" % h), A("TMPF", 512 * h, 512 * h + 512), ACT.Identity, -MEVEN)
+
+        hear(1, "Z2", A("MC", 7), NVB, after_relu2, evens)
 
     dma("Y", X(T.yf[:]), TBG, "dyf")
     keep_own(RO - 1, 1)
-    tt(A("TA", 0, 64), taken, A("SEL2"), mul)
-    red(A("RD", 2), A("TA", 0, 64), plus)
     ts(A("RD", 7), A("RD", 2), 32.0, mul)
     ts(A("OFFC"), A("CY"), A("RD", 7), plus)
     ts(A("OFFR", 0), A("RD", 7), D[13], plus, 8.0, plus)
     for b in range(2):
         arrive("NL%d" % (RO - 1), 32, 16 * b, 16, "an%d_%d" % (RO - 1, b), 1)
     cp(A("NLF"), A("NL%d" % (RO - 1)))
-    cp(A("DUP"), GI(A("NLF"), A("OFFC")))
-    cp(A("YR"), GI(A("NLF"), A("OFFR", 0)))
+    cp(A("DU2"), GI(A("NLF"), A("OFFC")))
+    cp(A("YQ"), GI(A("NLF"), A("OFFR", 0)))
+    cp(A("DUP"), GI(A("DU2"), A("OFFP")))
+    for b in range(2):
+        cp(A("YR", 8 * b, 8 * b + 8), A("YQ", b, 16, 2))
     tr(A("TRN"), A("DUP"))
     cp(A("YC"), GI(A("TRN"), A("OFFY")))
     dma("S", X(T.yr[:]), A("YR"), "dyr")

from concourse.bass import DstId, RemoteDMATransfer
from concourse.mybir import AluOpType as ALU, AxisListType as AX, ActivationFunctionType as ACT

N, W, RO = 8, 6144, 4
F, B, I, U = "float32", "bfloat16", "int32", "uint16"
NSAT = 4
G2, G3, G4 = 5, 2, 4
NVB = 11
CUTS = [0, 2, 6, 11, 14, 16]


def _scratch():
    s = {}
    for n, w, d in (
        ("TB", W + 1024, B), ("CLS", 128, I), ("RU", 16, B), ("L0", 128, U), ("CLF", 1024, F), ("TMPF", 1024, F),
        ("CL16", 1024, U), ("BI", 1024, I), ("PKI", 128, I), ("DUP", 256, F), ("TRN", 256, F), ("BL8", 128, B),
        ("IP", 2, I), ("CI", 8, I), ("CF", 8, F), ("D", 16, F), ("IOD", 16, F), ("IN", 144, F), ("IG", 128, F),
        ("IK", 128, F), ("IR", 128, F),
        ("E16", 144, B), ("EZ", 144, B), ("EM", 144, B), ("EP", 144, B), ("BLK", 128, B), ("RN", 64, B), ("CN", 64, B),
        ("CU", 128, B), ("MASKC", 32, F), ("CB", 16, F), ("SELB", 8, F), ("C8", 8, F), ("CY", 16, F),
        ("SEL1", 8, F), ("ID", 1024, B), ("MASK", 16, F), ("VO", 4, F), ("MR", 128, F), ("RST", 128, F), ("PN", 256, F),
        ("TA", 128, F), ("TC", 128, F),
        ("OFFD", 16, U), ("OFF0", 8, U), ("OFFY", 8, U), ("OFFU", 8, U), ("OFFC", 16, U), ("OFFR", 2, U),
        ("EQ", 2048, B), ("AB", 2048, B), ("JK", 128, B), ("RF", 16, F),
        ("PEN", 128, F), ("CM", 64, F), ("MN", 16, F), ("RD", 8, F), ("OS", 8, U), ("L16", 128, U),
        ("VV", 128, F), ("UI", 64, I), ("OO", 128, F),
        ("OF", 64, U), ("SG", 128, B),
        ("Z1", 1024, B), ("Z2", 1024, B), ("ZS", 1024, B), ("SJ", 1024, B), ("SS", 128, F), ("NI", 128, F), ("T1", 128, F), ("IB", 128, F),
        ("OFFP", 16, U), ("DU2", 256, F), ("YQ", 16, B), ("SC", 1032, B), ("PW", 8, F),
        ("RL", 1024, B), ("ZO", 1024, B), ("NE", 1024, B), ("NS", 1024, B), ("MC", 16, B), ("SCOL", 32, F),
        ("K1", 40, F), ("KD", 96, F), ("KE", 40, F), ("KJ", 2, U), ("KT", 96, F), ("KU", 40, F), ("BB", 16, F),
        ("NLF", 256, F), ("YC", 128, F), ("YR", 16, B),
    ):
        s[n] = ("sbuf", [128, w], d)
    s["IND"] = ("sbuf", [128, 12, 516], B)
    for n in range(RO):
        s["NL%d" % n] = ("sbuf", [128, 256], U)
        s["MSG%d" % n] = ("sbuf", [128, 16, 16], U)
        s["VL%d" % n] = ("sbuf", [128, 128], B)
        if n < RO - 1:
            s["PKL%d" % n] = ("sbuf", [128, 128], B)
    for n in ("KEY", "NR", "VC", "UU", "P20", "P21", "PV", "PP"):
        s[n] = ("psum", [128, 512], F)
    return s


SCRATCH = _scratch()
SEMAPHORES = (["sV", "sS", "sP", "sG", "loc", "ac", "hc", "dcl", "dru", "dfa", "dyf", "dyc", "dyr"]
              + ["an%d_%d" % (n, b) for n in range(RO) for b in range(2)] + ["av%d" % n for n in range(RO)]
              + [k + "%d" % n for k in ("ap", "hp") for n in range(RO - 1)])

KNEAR = float(2 ** 24 + 4)
MEVEN = 1.5 * 2 ** 24
UNDER = 1.0 - 2.0 ** -14
M1024 = 1.5 * 2 ** 33
BIG, FAR = 4096.0, 1048576.0
TINY = 2.0 ** -19


def _bits(cols):
    m = 0
    for c in cols:
        m |= 1 << c
    return m


def _helper(T, topo, r):
    c = T.cores[r]
    ok = [h for h in topo.cores_of(c) if T.rank_of(h) is None and all(topo.may_write(h, d) for d in T.cores)]
    return ([h for h in ok if topo.die(h) == topo.die(c)] + ok)[0]


def _far(T, topo, c, ranks):
    return [e for e in topo.engines(c, T.cores[ranks[0]]) if all(e in topo.engines(c, T.cores[r]) for r in ranks)]


def _dst(topo, c):
    rid, pid, _ = topo.addr(c)
    return DstId(rid=rid, pnc=pid)


def _copy_to(T, topo, cores, eng, sem, src, dst):
    return RemoteDMATransfer(dst_ids=[_dst(topo, c) for c in cores], dma_engine_mask=_bits(eng), remote_sem=T.sem[sem],
                             srcs=[src], dsts=[dst for c in cores])


def _handed(r):
    return [(r + d) % N for d in (5, 6, 7)]


def _hand_on(g, core, T, topo, r):
    peers = [p for p in range(N) if p != r]
    eng = _far(T, topo, core, peers)
    got = len(topo.engines(T.cores[r], core)) - len(_far(T, topo, T.cores[r], peers))
    jobs = [("hc", "ac", T.L0[:], T.CL16[:, 128 * r:128 * r + 128], _handed(r))]
    for n in range(RO - 1):
        ap = T["PKL%d" % n][:, 16 * r:16 * r + 16]
        jobs.append(("hp%d" % n, "ap%d" % n, ap, ap, peers))
    for sem, out, src, dst, to in jobs:
        g.wait_ge(T.sem[sem], got)
        g.remote_dma_fused([_copy_to(T, topo, [T.cores[p] for p in to], eng, out, src, dst)], local_sem=T.sem.loc)
    g.wait_ge(T.sem.loc, len(eng) * len(jobs))


def _emit(g, T, ops):
    queue = {"V": g.vector, "S": g.scalar, "P": g.tensor, "G": g, "Y": g.sync}
    hist = {}
    deps = []
    target = set()
    for i, o in enumerate(ops):
        d = set()
        for wr, regs in ((False, o["R"]), (True, o["W"])):
            for n, m in regs:
                ps = SCRATCH[n][0] == "psum"
                for j, w2, m2 in hist.get(n, ()):
                    same = ops[j]["q"] == o["q"]
                    if ps and not same:
                        d.add(j)
                    elif m & m2 and (wr or w2) and not (same and o["q"] == "P"):
                        d.add(j)
        for wr, regs in ((False, o["R"]), (True, o["W"])):
            for n, m in regs:
                h = hist.setdefault(n, [])
                if wr:
                    h[:] = [e for e in h if e[2] & ~m]
                h.append((i, wr, m))
        best = {}
        for j in d:
            if ops[j]["tok"] is None:
                best[ops[j]["q"]] = max(best.get(ops[j]["q"], -1), j)
        d = set(best.values()) | set(j for j in d if ops[j]["tok"] is not None)
        deps.append(d)
        target |= d
    last = {}
    count = {}
    known = {q: {} for q in queue}
    token = {}
    clock = {}
    for i, o in enumerate(ops):
        q = o["q"]
        if q is None:
            token[i] = o["tok"]
            clock[i] = {o["tok"][0]: o["tok"][1]}
            last[o["tok"][0]] = o["tok"][1]
            continue
        k = known[q]
        for j in sorted(deps[i], reverse=True):
            s, v = token[j]
            if k.get(s, 0) < v:
                queue[q].wait_ge(T.sem[s], v)
                for s2, v2 in clock[j].items():
                    k[s2] = max(k.get(s2, 0), v2)
        ins = o["fn"]()
        if o["tok"] is not None:
            s, v = o["tok"]
            if s != "loc":
                ins.then_inc(T.sem[s], 16)
        elif i in target:
            s = "s" + q
            count[s] = v = count.get(s, 0) + 1
            ins.then_inc(T.sem[s], 1)
        else:
            continue
        token[i] = (s, v)
        clock[i] = dict(k)
        clock[i][s] = v
        last[s] = v
    for s, v in last.items():
        if max(k.get(s, 0) for k in known.values()) < v:
            g.wait_ge(T.sem[s], v)


def rank_program(g, core, T, topo):
    me = T.rank_of(core)
    if me is None:
        for r in range(N):
            if _helper(T, topo, r) == core:
                _hand_on(g, core, T, topo, r)
        return
    ops = []
    peers = [r for r in range(N) if r != me]
    sent = [0]

    def A(n, lo=None, hi=None, st=1):
        if lo is None:
            w = 1
            for e in SCRATCH[n][1][1:]:
                w *= e
            return (T[n][:], [(n, (1 << w) - 1)], [])
        if hi is None:
            hi = lo + 1
        ap = T[n][:, lo:hi] if st == 1 else T[n][:, lo:hi:st]
        return (ap, [(n, _bits(range(lo, hi, st)))], [])

    def A3(n, rows, cols):
        h, w = SCRATCH[n][1][1:]
        cs = [cols] if isinstance(cols, int) else range(w)[cols]
        rs = [rows] if isinstance(rows, int) else range(h)[rows]
        return (T[n][:, rows, cols], [(n, _bits(r * w + c for r in rs for c in cs))], [])

    def top(n, p, w):
        return (T[n][0:p, 0:w], [(n, (1 << w) - 1)], [])

    def GI(win, off):
        return (win[0].indirect(off[0]), win[1], off[1])

    def add(q, fn, outs, ins, tok=None):
        rd, wr = [], []
        for x in ins:
            if isinstance(x, tuple):
                rd += x[1] + x[2]
        for x in outs:
            wr += x[1]
            rd += x[2]
        ops.append({"q": q, "fn": fn, "R": rd, "W": wr, "tok": tok})

    def P(x):
        return x[0] if isinstance(x, tuple) else x

    def ts(o, a, s1, op0, s2=None, op1=None):
        if op1 is None:
            add("V", lambda: g.vector.tensor_scalar(o[0], a[0], P(s1), None, op0), [o], [a, s1])
        else:
            add("V", lambda: g.vector.tensor_scalar(o[0], a[0], P(s1), P(s2), op0, op1), [o], [a, s1, s2])

    def tt(o, a, b, op):
        add("V", lambda: g.vector.tensor_tensor(o[0], a[0], b[0], op), [o], [a, b])

    def cp(o, a):
        add("V", lambda: g.vector.tensor_copy(o[0], a[0]), [o], [a])

    def red(o, a, op, neg=False, ab=False):
        add("V", lambda: g.vector.tensor_reduce(o[0], a[0], AX.X, op, negate=neg, apply_absolute_value=ab), [o], [a])

    def scan(o, d0, d1, init, op0, op1):
        add("V", lambda: g.vector.tensor_tensor_scan(o[0], d0[0], d1[0], P(init), op0, op1), [o], [d0, d1, init])

    def tr(o, a):
        add("V", lambda: g.vector.transpose(o[0], a[0]), [o], [a])

    def ms(o, v):
        add("V", lambda: g.vector.memset(o[0], v), [o], [])

    def act(o, a, f, bias=0.0, scale=1.0, acc=None):
        if acc is None:
            add("S", lambda: g.scalar.activation(o[0], a[0], f, bias=P(bias), scale=P(scale)), [o], [a, bias, scale])
        else:
            add("S", lambda: g.scalar.activation(o[0], a[0], f, bias=P(bias), scale=scale, accum_out=acc[0]),
                [o, acc], [a, bias])

    def mm(o, l, r, start, stop):
        add("P", lambda: g.tensor.matmul(o[0], l[0], r[0], start, stop), [o], [l, r])

    def iota(o, pat, cm=0):
        if SCRATCH[o[1][0][0]][2] == I:
            add("G", lambda: g.iota(o[0], pat, 0, cm), [o], [])
        else:
            add("G", lambda: g.iota(o[0], pat, 0, cm, allow_small_or_imprecise_dtypes=True), [o], [])

    def dma(q, o, a, sem):
        e = g.sync if q == "Y" else g.scalar
        add(q, lambda: e.dma_start(o[0], a[0]), [o], [a], (sem, 16))

    def X(ap):
        return (ap, [], [])

    eng = _far(T, topo, core, peers)
    helper = _helper(T, topo, me)
    near = [e for e in topo.engines(core, helper) if e not in eng]

    def send(src, parts):
        sent[0] += sum(len(p[1]) for p in parts)
        ts_ = [_copy_to(T, topo, cores, e, sem, src[0], to) for cores, e, sem, to in parts]
        add("G", lambda: g.remote_dma_fused(ts_, local_sem=T.sem.loc), [], [src], ("loc", sent[0]))

    def send_each(n, b):
        sent[0] += len(peers)
        w = 16 if n == RO - 1 else 10
        src = [A3("MSG%d" % n, 2 * r + b, slice(0, w)) for r in peers]
        c = 16 * (2 * me + b)
        ts_ = [RemoteDMATransfer(dst_ids=[_dst(topo, T.cores[r])], dma_engine_mask=1 << eng[i],
                                 remote_sem=T.sem["an%d_%d" % (n, b)], src=src[i][0], dst=T["NL%d" % n][:, c:c + w])
               for i, r in enumerate(peers)]
        add("G", lambda: g.remote_dma_fused(ts_, local_sem=T.sem.loc), [], src, ("loc", sent[0]))

    def arrive(n, step, lo, w, sem, per):
        ops.append({"q": None, "fn": None, "R": [],
                    "W": [(n, _bits(range(r * step + lo, r * step + lo + w))) for r in peers],
                    "tok": (sem, per * len(peers))})

    def WQ(n, q):
        return A(n, 15 - q, 143 - q)

    mul, sub, eq_, plus = ALU.mult, ALU.subtract, ALU.is_equal, ALU.add
    shr, band = ALU.logical_shift_right, ALU.bitwise_and
    TBG = A("TB", 0, W)
    allc, all64 = slice(0, 16), slice(0, 64)

    dma("Y", A("CLS"), X(T.cl[:]), "dcl")
    dma("S", A("RU"), X(T.ru[:]), "dru")
    dma("Y", TBG, X(T.fa[:]), "dfa")
    iota(A("IP", 0), [[0, 1]], 1)
    iota(A("IOD"), [[16, 8], [0, 2]])
    iota(A("IN"), [[1, 144]])
    iota(A("IG"), [[1, 8], [0, 16]])
    iota(A("IR"), [[0, 16], [1, 8]])
    iota(A("IB"), [[2, 8], [0, 8], [1, 2]])
    ms(A("CB", 0), 0.0)
    ms(A("CB", 1), 64.0 - KNEAR)
    ms(A("CB", 2, 16), 0.0)
    for c, (sh, m) in enumerate(((4, 7), (0, 15), (4, 1), (3, 1), (0, 7), (0, 1), (1, 7), (1, 1))):
        ts(A("CI", c), A("IP", 0), sh, shr, m, band)
    ms(A("CN"), 23.0 / 2048)
    cp(A("CF"), A("CI"))
    pg, x, ga, xh, xl, xb, x2, xc = [A("CF", c) for c in range(8)]
    D = [A("D", c) for c in range(16)]
    ms(A("PEN", 7, 128, 8), 0.0)
    ts(A("OFFD"), A("IOD"), x, plus)
    ts(D[8], xl, 4.0, mul, xh, plus)
    ts(D[1], pg, 16.0, mul, 15.0, plus)
    ts(D[0], ga, 2.0, mul, D[8], plus)
    ts(A("TA", 8, 16), A("IN", 0, 8), 1.0 / 8, mul)
    ts(A("OFF0"), A("TA", 8, 16), D[0], plus, 8.0, mul)
    for n in range(RO):
        ms(A("MSG%d" % n), 0)
    cp(A("DUP"), GI(A("CLS"), A("OFFD")))
    tr(A("TRN"), A("DUP"))
    cp(A("L0"), GI(A("TRN"), A("OFF0")))
    send(A("L0"), [([T.cores[r] for r in peers if r not in _handed(me)], eng, "ac", T.CL16[:, 128 * me:128 * me + 128]),
                   ([helper], near, "hc", T.L0[:])])
    ts(A("E16"), A("IN"), D[1], eq_, 1.0 / 16, mul)
    ts(D[3], ga, 16.0, mul, x, plus)
    ts(D[4], xb, 8.0, mul)
    ts(D[5], x2, -7.0, plus, BIG, mul)
    ts(D[6], x, 64.0, mul)
    ts(D[7], pg, 2.0, mul, xb, plus)
    ts(D[10], xc, -1.0, plus, 1.0 / 16, mul)
    ts(D[11], xc, -32.0, mul)
    ts(D[13], xb, 16.0, mul)
    ts(D[14], xb, 8.0, mul, x2, plus)
    ts(D[2], xl, 2.0, mul, xh, plus)
    ts(A("MASK"), A("IR", 0, 16), x2, eq_)
    ts(A("BLK"), A("IG"), pg, eq_, -4.0, mul)
    ts(A("BL8"), A("IB"), D[7], eq_, -4.0, mul)
    ts(A("OFFP"), A("IN", 0, 16), 16.0, mul, D[2], plus)
    ts(A("CU"), A("IG"), D[10], mul, D[11], plus)
    ts(A("TA", 0, 8), A("IN", 0, 8), 128.0, mul, D[14], plus)
    ts(A("KT", 0, 32), A("IG", 0, 32), ga, ALU.not_equal, float(2 ** 22), mul)
    ms(A("KEY", 64, 96), 2.0 ** 23)
    ms(A("KD", 0, 64), 0.0)
    ms(A("TC", 0, 6), 0.5)
    ms(A3("IND", slice(1, 12, 2), 512), 0.0)
    ms(A3("IND", slice(1, 12, 2), 514), 0.0)
    scan(A("PW", 0, 6), A("TC", 0, 6), A("KD", 0, 6), 64.0, mul, plus)
    for h, c, f in ((0, 512, 2.0 ** -11), (0, 513, 1.5 * 2 ** 23), (0, 514, 0.5), (1, 513, -1.5 * 2 ** 23)):
        ts(A3("IND", slice(h, 12, 2), c), A("PW", 0, 6), f, mul)
    ms(A("KE", 0, 32), 0.0)
    ms(A("KE", 32), -511.5)
    ms(A("KE", 33), M1024)
    ms(A("KE", 34), -M1024)
    ms(A("KU", 32, 35), 4 * M1024)
    ts(A("EZ"), A("IN"), D[1], eq_, 1024.0, mul)
    ts(A("EM"), A("IN"), D[1], eq_, -2048.0, mul)
    ts(A("EP"), A("IN"), D[1], eq_, 2048.0, mul)
    ts(A("RN"), A("IN", 0, 64), -1.0 / 64, mul)
    ts(A("SELB"), A("TA", 0, 8), 112.0, plus, 256.0, mul)
    ts(A("MASKC"), A("KT", 0, 32), D[6], plus)
    cp(A("KD", 64), A("MASKC", 0))
    tt(A("KD", 65, 96), A("MASKC", 1, 32), A("MASKC", 0, 31), sub)
    ts(A("C8"), A("IN", 0, 8), D[4], plus, 1.0 / 16, mul)
    ts(A("CY"), A("IOD"), 1.0 / 16, mul, D[13], plus)
    ts(A("OFFY"), A("IN", 0, 8), 32.0, mul, D[3], plus)
    ts(A("SEL1"), A("IN", 0, 8), x2, eq_, 1.0 / BIG, mul)
    ts(D[9], pg, 16.0, mul, x, plus)
    for s in range(8):
        ts(A("ID", 128 * s, 128 * s + 128), A("IN", 0, 128), D[9], eq_, 2.0 ** (7 - s), mul)
    ts(A("RST"), A("IR"), 0.0, ALU.is_gt, -FAR, mul)
    cp(A("CL16", 128 * me, 128 * me + 128), A("L0"))
    ms(A("PN", 0, 256, 2), -1.0)
    ts(A("NR", 1, 128, 2), A("IN", 0, 64), D[6], plus, -TINY, mul)
    ts(A("NR", 1, 128, 2), A("NR", 1, 128, 2), -TINY * W, plus)

    def keep_own(n, b):
        c = 16 * (2 * me + b)
        cp(A("NL%d" % n, c, c + 16), A3("MSG%d" % n, 2 * me + b, allc))

    def rulings(n, b):
        arrive("NL%d" % n, 32, 16 * b, 10, "an%d_%d" % (n, b), 1)
        cp(A("RF", 8 * b, 8 * b + 8), A("NL%d" % n, 16 * b + 8, 256, 32))

    heard = A("MR", 7, 128, 16)

    for n in range(RO):
        final = n == RO - 1
        NL, MSG, pn = "NL%d" % n, "MSG%d" % n, "NL%d" % (n - 1)

        slot = list(range(8)) + [8 + me] + [8 + r for r in peers]

        def names(s):
            c = 16 * (slot[s] % 8) + 8 * (slot[s] // 8)
            return A("L0", c, c + 8) if n == 0 else A(pn, 2 * c, 2 * c + 8)

        def rul(s):
            return A("RU", slot[s]) if n == 0 else A("BB", 0) if s == 8 else A("RF", slot[s])

        def count(lo, hi):
            for s in range(lo, hi):
                mm(A("VC", 0, 128), WQ("E16", 2 * (slot[s] % 8) + slot[s] // 8), A("EQ", 128 * s, 128 * s + 128),
                   s == 0, s == 15)

        def vgather(s):
            ts(A("EQ", 128 * s, 128 * s + 128), GI(TBG, names(s)), rul(s), ALU.not_equal)
            count(s, s + 1)

        def sgather(lo, hi):
            for s in range(lo, hi):
                act(A("AB", 128 * s, 128 * s + 128), GI(TBG, names(s)), ACT.Abs, rul(s), -1.0)

        def cut(lo, hi):
            ts(A("EQ", 128 * lo, 128 * hi), A("AB", 128 * lo, 128 * hi), 1.0, ALU.min)
            count(lo, hi)

        VL = "VL%d" % n
        mm(A("UU", 0, 128), A("BL8"), A("CU"), True, False)
        if n > 0:
            keep_own(n - 1, 1)
        sgather(3, 8)
        for s in (0, 1, 2, 8):
            vgather(s)
        cut(3, 6)
        if n > 0:
            rulings(n - 1, 1)
        sgather(13, 16)
        cut(6, 8)
        for s in (9, 10, 11):
            vgather(s)
        cut(13, 15)
        vgather(12)
        cut(15, 16)
        act(A("JK"), A("VC", 0, 128), ACT.Sign, 7.5 / 16, -1.0, A("VO", 0))
        src = A(VL, 16 * me, 16 * me + 16)
        act(src, A("MASK"), ACT.Identity, 0.0, A("VO", 0))
        send(src, [([T.cores[r] for r in peers], eng, "av%d" % n, src[0])])
        if n == 0:
            arrive("CL16", 128, 0, 128, "ac", len(eng))
            cp(A("CLF"), A("CL16"))
        else:
            pk = "PKL%d" % (n - 1)
            arrive(pk, 16, 0, 16, "ap%d" % (n - 1), len(eng))
            ts(A("PKI"), GI(A(pk), A("OFFU")), 255.0, plus, 0.5, mul)
            for s in range(8):
                ts(A("BI", s, 1024, 8), A("PKI"), 7 - s, shr, 1, band)
            for h in range(2):
                tt(A("CLF", 512 * h, 512 * h + 512), A("BI", 512 * h, 512 * h + 512), A("P2%d" % h), plus)
        arrive(VL, 16, 0, 16, "av%d" % n, len(eng))
        mm(A("UU", 0, 128), A("BL8"), A(VL), False, True)
        for i in range(7):
            key, pen = [lambda j: A("UU", j, 128, 8), lambda j: A("PEN", j, 128, 8)]
            high, down = [lambda j: key(j) if j < 2 else A("CM", 32 * (j % 2), 32 * (j % 2) + 16),
                        lambda j: key(j) if j < 2 else A("CM", 32 * (j % 2) + 16, 32 * (j % 2) + 32)]
            if i == 0:
                red(A("MN", 15), A("UU", 0, 128, 16), ALU.min)
            else:
                scan(A("MN"), high(i), pen(i - 1), FAR, sub, ALU.max)
            if 1 <= i <= 5:
                tt(high(i + 1), key(i + 1), pen(i - 1), sub)
            ts(pen(i), down(i), A("MN", 15), ALU.is_le, -BIG * (7 - i), mul)
            if 1 <= i <= 5:
                tt(down(i + 1), key(i + 1), pen(i - 1), plus)
        red(A("RD", 0), A("PEN", 16 * me, 16 * me + 8), ALU.min)
        ts(A("OS"), A("SELB"), A("RD", 0), plus, 1.0 / 256, mul)
        cp(A("NI"), GI(A("CLF"), A("OS")))

        def H(k, b):
            return A(k, 64 * b, 64 * b + 64)

        def NH(k, b):
            return A(k, b, 128, 2)

        for b in range(2):
            cp(H("L16", b), NH("NI", b))

        def gather(zn, b):
            act(A(zn, 512, 1024), GI(TBG, A("L16", 64 * b + 32, 64 * b + 64)), ACT.Identity)
            cp(A(zn, 0, 512), GI(TBG, A("L16", 64 * b, 64 * b + 32)))

        def key_open(zn):
            mm(A("KEY", 0, 64), A("BLK"), A("RN"), True, False)
            for q in range(16):
                mm(A("KEY", 0, 64), WQ("EZ", q), A(zn, 64 * q, 64 * q + 64), False, False)
            mm(A("NR", 0, 128, 2), A("BLK"), A("CN"), True, False)

        def sstep(i):
            nb = -31.5 if i == 0 else A("SCOL", 15 + i)
            act(A("SJ"), A("ZS"), ACT.Sign, nb, 1.0, A("SCOL", i))
            act(A("SCOL", 8 + i), A("SCOL", i), ACT.Sign, 1.0)
            act(A("SCOL", 16 + i), A("SCOL", 8 + i), ACT.Identity, nb, -16.0 / 2 ** i)

        def lift(zn, lo, hi):
            ts(A("ZO", 16 * lo, 16 * hi), A(zn, 16 * lo, 16 * hi), 64.0, plus)

        def half(h, i=0, w=512):
            return A3("IND", 2 * i + h, slice(0, w))

        def slift(zn, lo, hi):
            act(A("ZO", 16 * lo, 16 * hi), A(zn, 16 * lo, 16 * hi), ACT.Identity, 64.0)

        side = [[lambda b=b: ts(H("PV", b), NH("T1", b), -MEVEN, plus, 0.5, plus),
                 lambda b=b: ts(A("PN", 128 * b + 1, 128 * b + 128, 2), NH("NI", b), -TINY, mul),
                 lambda b=b: tt(H("SS", b), NH("NI", b), H("PV", b), sub)] for b in range(2)]
        lifts = [lambda i=i: lift("Z1", 8 * i, 8 * i + 8) for i in range(8)]
        slots = [lambda: scan(A("MR"), A("RST"), A("PEN"), 0.0, ALU.max, ALU.min),
                 lambda: tt(A("TC", 0, 8), heard, A("SEL1"), mul),
                 lambda: ts(A("TA", 0, 8), heard, D[5], eq_),
                 lambda: red(A("RD", 4), A("TC", 0, 8), plus),
                 lambda: tt(A("TA", 8, 16), A("TA", 0, 8), A("IN", 0, 8), mul),
                 lambda: ts(A("MASK"), A("IR", 0, 16), A("RD", 4), sub, 7.0, eq_),
                 lambda: red(A("RD", 2), A("TA", 8, 16), plus),
                 lambda: ts(A("OFFU"), A("C8"), A("RD", 2), plus, 16.0, mul)]

        later = [side[0][0], side[1][0], side[0][1], side[0][2], side[1][2], side[1][1]] + slots

        def gap(k=1):
            for f in later[:k]:
                f()
            del later[:k]

        act(A("T1"), A("NI"), ACT.Identity, MEVEN, UNDER)
        gather("Z1", 0)
        act(A("ZS"), GI(TBG, A("L16", 64, 128)), ACT.Identity)
        key_open("Z1")
        for i in range(NSAT):
            sstep(i)
        for i in range(6):
            o = 516 * (i % 2)
            if i == 0:
                for h in range(2):
                    ts(half(h), A("Z1", 512 * h, 512 * h + 512), 32.0, ALU.is_ge, 2.0 ** -5, mul)
            else:
                ts(A3("IND", slice(2 * i, 2 * i + 2), slice(0, 512)), A("Z1"), A("SC", 516 - o + 514), ALU.is_ge,
                   2.0 ** (-5 - i), mul)
            scan(A("SC", o, o + 515), half(0, i, 515), half(1, i, 515),
                 0.0 if i == 0 else A("SC", 516 - o + 513), plus, plus)

        def hear(b, zn, med, nv, after_relu, after_sign):
            cuts = CUTS if nv == 16 else [0, 2, 5, 8, nv]
            for lo, hi in zip(cuts, cuts[1:]):
                ts(A("RL", 64 * lo, 64 * hi), A(zn, 64 * lo, 64 * hi), med, sub, 0.0, ALU.min)
            if nv < 16:
                act(A("RL", 64 * nv, 1024), A(zn, 64 * nv, 1024), ACT.Relu, med, -1.0)
            order = list(range(8)) + list(range(nv, 16)) + list(range(8, nv))
            for q in order:
                mm(A("KEY", 0, 64), WQ("EM" if q < nv else "EP", q), A("RL", 64 * q, 64 * q + 64), False, q == order[-1])
            after_relu()
            scan(A("KT"), A("KD"), A("KEY", 0, 96), 2.0 ** 23, plus, ALU.min)
            tr(A("KU", 0, 32), A("KT", 64, 96))
            scan(A("K1", 0, 35), A("KE", 0, 35), A("KU", 0, 35), 2.0 ** 23, plus, ALU.min)
            ts(A("KJ", 0), A("K1", 31), A("K1", 34), sub)
            tt(A("BB"), GI(A(zn), A("KJ", 0)), A("CB"), plus)
            parts = ((0, 8), (1, 4), (2, 4), (3, 4), (4, 8))
            for c, st in parts:
                ts(A("NE", c, 1024, st), A("ZO", c, 1024, st), A("BB", 1), sub, KNEAR, eq_)
            act(A("NS"), A(zn), ACT.Sign, A("BB", 0), -1.0)
            order = [q for c, st in parts for q in range(c, 16, st)]
            for q in order:
                mm(A("NR", 0, 128, 2), WQ("E16", q), A("NE", q, 1024, 16), False, q == order[-1])
            cp(A3(MSG, slice(b, 16, 2), 8), A("BB", 2, 10))
            if b == 1 and not final:
                rulings(n, 0)
            gap(G2 if b == 0 else 9)
            vv = A("VV", 64 * b, 64 * b + 64)
            f1 = lambda: scan(A("OO"), A("PN", 128 * b, 128 * b + 128), A("NR", 0, 128), 0.0, ALU.min, ALU.max)
            f2 = lambda: ts(A("OF"), A("OO", 1, 128, 2), -1.0 / TINY, mul)
            v1 = lambda: tt(vv, A("NR", 0, 128, 2), H("SS", b), mul)
            v2 = lambda: tt(A("UI"), vv, H("PV", b), plus)
            v3 = lambda: cp(A3(MSG, slice(b, 16, 2), slice(0, 8)), A("UI"))
            sc = lambda: tt(GI(A("TB"), A("OF")), A(zn), A("NS"), plus)
            for f in (v1, f1, v2, f2, v3):
                f()
            send_each(n, b)
            if b == 1 and not final:
                act(H("SG", b), vv, ACT.Sign)
                pk = A("PKL%d" % n, 16 * me, 16 * me + 16)
                for s in range(8):
                    mm(A("PP", 0, 16), A("ID", 128 * s, 128 * s + 128), A("SG", s, 128, 8), s == 0, s == 7)
                act(pk, A("PP", 0, 16), ACT.Identity)
                send(pk, [([helper], near, "hp%d" % n, pk[0])])
            after_sign()
            sc()

        def s_finish():
            for i in range(NSAT, 6):
                sstep(i)
            act(A("MC", 0), A("SCOL", 21), ACT.Identity, -1.0, -1.0)
            act(A("SCOL", 24), A("SCOL", 21), ACT.Identity, -0.5)
            if not final:
                act(H("SG", 0), H("VV", 0), ACT.Sign)

        hear(0, "Z1", A("SC", 516 + 513), 16, lambda: lift("Z1", 0, 64), s_finish)
        gather("Z2", 1)
        key_open("Z2")
        for h in range(2):
            ts(half(h, 5), A("Z2", 512 * h, 512 * h + 512), A("MC", 0), ALU.is_gt, 2.0 ** -10, mul)
        keep_own(n, 0)
        act(A("SJ"), A("Z2"), ACT.Sign, A("SCOL", 24), 1.0, A("SCOL", 26))
        scan(A("SC", 0, 515), half(0, 5, 515), half(1, 5, 515), A("MC", 0), plus, plus)
        gap(G3)
        ts(A("MC", 7), A("SCOL", 26), 0.0, ALU.is_ge, A("SC", 513), plus)

        def after_relu2():
            lift("Z2", 0, 24)
            slift("Z2", 24, 64)
            gap(G4)

        def evens():
            if n == 0:
                act(A("TMPF"), A("CLF"), ACT.Identity, MEVEN, UNDER)
                for h in range(2):
                    act(A("P2%d" % h), A("TMPF", 512 * h, 512 * h + 512), ACT.Identity, -MEVEN)

        hear(1, "Z2", A("MC", 7), NVB, after_relu2, evens)

    dma("Y", X(T.yf[:]), TBG, "dyf")
    keep_own(RO - 1, 1)
    ts(A("RD", 7), A("RD", 2), 32.0, mul)
    ts(A("OFFC"), A("CY"), A("RD", 7), plus)
    ts(A("OFFR", 0), A("RD", 7), D[13], plus, 8.0, plus)
    for b in range(2):
        arrive("NL%d" % (RO - 1), 32, 16 * b, 16, "an%d_%d" % (RO - 1, b), 1)
    cp(A("NLF"), A("NL%d" % (RO - 1)))
    cp(A("DU2"), GI(A("NLF"), A("OFFC")))
    cp(A("YQ"), GI(A("NLF"), A("OFFR", 0)))
    cp(A("DUP"), GI(A("DU2"), A("OFFP")))
    for b in range(2):
        cp(A("YR", 8 * b, 8 * b + 8), A("YQ", b, 16, 2))
    tr(A("TRN"), A("DUP"))
    cp(A("YC"), GI(A("TRN"), A("OFFY")))
    dma("S", X(T.yr[:]), A("YR"), "dyr")
    dma("S", X(T.yc[:]), A("YC"), "dyc")
    _emit(g, T, ops)
